import numpy as np
import ml_dtypes


def mxq(x, axis, fmt="e4m3"):
    dtype, down = {"e4m3": (ml_dtypes.float8_e4m3fn, 7), "e5m2": (ml_dtypes.float8_e5m2, 14)}[fmt]
    v = np.moveaxis(np.asarray(x, np.float32).astype(ml_dtypes.bfloat16).astype(np.float64), axis, -1)
    blocks = v.reshape(v.shape[:-1] + (-1, 32))
    amax = np.abs(blocks).max(-1, keepdims=True)
    byte = np.maximum(np.where(amax > 0, np.frexp(amax)[1] - 1 + 127, 0) - down, 1)
    scale = np.exp2(byte - 127.0)
    codes = (blocks / scale).astype(np.float32).astype(dtype).astype(np.float64)
    return np.moveaxis((codes * scale).reshape(v.shape), -1, axis)


WIDE = False


def mx_kscale(k):
    if not WIDE:
        return np.ones(k)
    levels = np.array([10, -10, 5, -5, 0])
    if k % 512:
        return np.exp2(np.random.permutation(np.resize(levels, k // 32))).repeat(32)
    a = np.empty((k // 512, 16))
    for p in range(k // 512):
        a[p, :8] = np.random.permutation(np.resize(levels, 8))
        for g in range(8):
            far = levels[np.abs(levels - a[p, g]) >= 10]
            a[p, g + 8] = far[np.random.randint(len(far))]
    return np.exp2(a.ravel()).repeat(32)


BF16 = ml_dtypes.bfloat16


def bf(x):
    return np.asarray(x, np.float32).astype(BF16)


def f64(x):
    return np.asarray(x).astype(np.float64)


E2M1 = np.array([0.0, 0.5, 1.0, 1.5, 2.0, 3.0, 4.0, 6.0, -0.0, -0.5, -1.0, -1.5, -2.0, -3.0, -4.0, -6.0])


def pack_weight(w, fmt):
    k, n = w.shape
    w = f64(bf(w)).reshape(k // 32, 32, n)
    amax = np.abs(w).max(1)
    if fmt == "e4m3":
        byte = np.frexp(amax)[1] - 1 + 127 - 7
    else:
        mant, ex = np.frexp(amax / 6.0)
        byte = np.where(mant > 0.5, ex, ex - 1) + 127
    byte = np.clip(np.where(amax > 0, byte, 1), 1, 254)
    scaled = (w * np.exp2(127.0 - byte)[:, None, :]).reshape(k, n).astype(np.float32)
    by_word = np.ascontiguousarray(scaled.reshape(k // 512, 128, 4, n).transpose(0, 1, 3, 2))
    if fmt == "e4m3":
        words = by_word.astype(ml_dtypes.float8_e4m3fn).view(np.uint8)
    else:
        c = by_word.astype(ml_dtypes.float4_e2m1fn).view(np.uint8) & 0xF
        words = c[..., 0::2] | (c[..., 1::2] << 4)
    return np.ascontiguousarray(words), np.ascontiguousarray(byte.astype(np.uint8).reshape(k // 512, 16, n))


def unpack_weight(words, scales, fmt):
    g, p, n, _ = words.shape
    if fmt == "e4m3":
        vals = np.ascontiguousarray(words).view(ml_dtypes.float8_e4m3fn).astype(np.float64)
    else:
        nib = np.empty((g, p, n, 4), np.uint8)
        nib[..., 0::2] = words & 0xF
        nib[..., 1::2] = words >> 4
        vals = E2M1[nib]
    vals = vals * np.repeat(np.exp2(scales.astype(np.float64) - 127.0), 8, axis=1)[..., None]
    return vals.transpose(0, 1, 3, 2).reshape(g * 512, n)
def pack4(w):
    words, scales = pack_weight(w, "e2m1")
    return words.reshape(words.shape[0], 128, -1), scales


def unpack4(words, scales):
    return unpack_weight(words.reshape(words.shape[0], 128, -1, 2), scales, "e2m1")


M, A, B, N = 1024, 512, 1536, 2048

TAU = 0.04


def setup_inputs():
    s, t = mx_kscale(A), mx_kscale(B)
    size = np.exp(0.3 * np.random.standard_normal((M, 1)))
    hi = 2.0 * size * np.random.standard_normal((M, A))
    lo = size * np.random.standard_normal((M, B))
    norm = np.sqrt((hi * hi).sum(1) + (lo * lo).sum(1))
    w_hi = np.random.standard_normal((A, N)) / np.sqrt(A + B)
    w_lo = np.random.standard_normal((B, N)) / np.sqrt(A + B)
    w_lo_words, w_lo_scales = pack4(w_lo / t[:, None])
    return {"z_hi": bf(hi * s),
            "z_lo": bf(lo * t),
            "w_hi": bf(w_hi / s[:, None]),
            "w_lo_words": w_lo_words,
            "w_lo_scales": w_lo_scales,
            "sharpen": bf(1.0 / (norm * TAU)),
            "centre": bf(0.3 * np.random.standard_normal(N))}


def reference(z_hi, z_lo, w_hi, w_lo_words, w_lo_scales, sharpen, centre):
    u = ((mxq(f64(z_hi), 1, "e4m3") @ mxq(f64(w_hi), 0, "e4m3"))
         + (mxq(f64(z_lo), 1, "e4m3") @ unpack4(w_lo_words, w_lo_scales)))
    logits = u * f64(sharpen)[:, None] - f64(centre)[None, :]
    return np.exp(logits)

@@ -1,0 +1,523 @@
+from contextlib import ExitStack
+
+import concourse.mybir as mybir
+from concourse.masks import make_identity
+
+M, A, B, N = 1024, 512, 1536, 2048
+FLOPS = 2 * M * (A + B) * N
+
+F32 = mybir.dt.float32
+BF16 = mybir.dt.bfloat16
+I32 = mybir.dt.int32
+U32 = mybir.dt.uint32
+U8 = mybir.dt.uint8
+FP8X4 = mybir.dt.float8_e4m3fn_x4
+FP4X4 = mybir.dt.float4_e2m1fn_x4
+MULT = mybir.AluOpType.mult
+SUB = mybir.AluOpType.subtract
+EXP = mybir.ActivationFunctionType.Exp
+
+P = 128
+R = M // P
+C = 4
+W = N // C
+G = B // 512
+LOADS = "a0 l0 s0 b0 l1 h0 l2 w0 z1 h1 w1 w2 w3 z2 h2 z3 h3 z4 h4 z5 h5 z6 h6 z7 h7"
+STR = (0, 1)
+HI = G
+
+
+def tile_dino_teacher_scores_s1_kernel(tc, z_hi, z_lo, w_hi, w_lo_words, w_lo_scales, sharpen, centre, out):
+    nc = tc.nc
+    with ExitStack() as ctx:
+        keep = ctx.enter_context(tc.tile_pool(name="keep", bufs=1))
+        work = ctx.enter_context(tc.tile_pool(name="work", bufs=3))
+        outs = ctx.enter_context(tc.tile_pool(name="outs", bufs=12))
+        psum = ctx.enter_context(tc.psum_pool(name="psum", bufs=1))
+
+        ident = keep.tile([P, P], F32, name="ident", align_bytes=64)
+        make_identity(nc, ident[:])
+        ident_b = keep.tile([P, P], BF16, name="ident_b", align_bytes=64)
+        vecs = keep.tile([P, P], BF16, name="vecs", align_bytes=64)
+        sharp = keep.tile([P, R], F32, name="sharp", align_bytes=64)
+        ccol = keep.tile([P, N // P], BF16, name="ccol", align_bytes=64)
+        cbc = keep.tile([P, N], BF16, name="cbc", align_bytes=64)
+        junk = keep.tile([P, 1], F32, name="junk", align_bytes=64)
+        wls = keep.tile([P, G, N], U8, name="wls", align_bytes=64)
+        wlo = []
+        for g in range(G):
+            t = keep.tile([P, 2 * N], U8, name="wlo%d" % g, align_bytes=64)
+            wlo.append(t)
+        whr, whc, whs = [], [], []
+        for c in range(C):
+            t = keep.tile([P, 4, W], BF16, name="whr%d" % c, align_bytes=64)
+            whr.append(t)
+            t = keep.tile([P, W], U32, name="whc%d" % c, align_bytes=64)
+            whc.append(t)
+            t = keep.tile([P, W], U8, name="whs%d" % c, align_bytes=64)
+            whs.append(t)
+        zlo, zhi, zc, zs = [], [], [], []
+        for r in range(R):
+            t = keep.tile([P, B], BF16, name="zlo%d" % r, align_bytes=64)
+            zlo.append(t)
+            t = keep.tile([P, A], BF16, name="zhi%d" % r, align_bytes=64)
+            zhi.append(t)
+            t = keep.tile([P, 4 * P], U32, name="zc%d" % r, align_bytes=64)
+            zc.append(t)
+            t = keep.tile([P, 4 * P], U8, name="zs%d" % r, align_bytes=64)
+            zs.append(t)
+        rows = [slice(r * P, (r + 1) * P) for r in range(R)]
+
+        ctx.enter_context(tc.manual_schedule())
+
+        nc.vector.memset(vecs[:].bitcast(I32), 0)
+        nc.vector.memset(junk[:], 0.0)
+        nc.vector.memset(wls[:].rearrange("p g n -> p (g n)").bitcast(I32), 0)
+        nc.vector.tensor_copy(out=ident_b[:], in_=ident[:])
+        nc.scalar.dma_start(out=vecs[0:16, :], in_=centre.rearrange("(a b) -> a b", b=P))
+        nc.scalar.dma_start(out=vecs[16:24, :], in_=sharpen.rearrange("(a b) -> a b", b=P))
+        nc.scalar.activation(out=junk[:], in_=junk[:], func=EXP)
+
+        def load_wlo(g):
+            nc.sync.dma_start(out=wlo[g][:].bitcast(I32), in_=w_lo_words[g].bitcast(I32))
+
+        wh_view = w_hi.rearrange("(p j) n -> p j n", j=4)
+        for tok in LOADS.split():
+            k, i = tok[0], int(tok[1:])
+            if k == "l":
+                load_wlo(i)
+            elif k == "s":
+                for q in range(4):
+                    nc.sync.dma_start(
+                        out=wls[32 * q : 32 * q + 4, :, :].bitcast(I32),
+                        in_=w_lo_scales[:, 4 * q : 4 * q + 4, :].rearrange("g r n -> r g n").bitcast(I32),
+                    )
+            elif k == "a":
+                nc.sync.dma_start(out=zlo[i][:, 0:512], in_=z_lo[rows[i], 0:512])
+            elif k == "b":
+                nc.sync.dma_start(out=zlo[i][:, 512:B], in_=z_lo[rows[i], 512:B])
+            elif k == "z":
+                nc.sync.dma_start(out=zlo[i][:], in_=z_lo[rows[i], :])
+            elif k == "h":
+                nc.sync.dma_start(out=zhi[i][:], in_=z_hi[rows[i], :])
+            else:
+                nc.sync.dma_start(out=whr[i][:], in_=wh_view[:, :, i * W : (i + 1) * W])
+
+        pre, grp, xts = {}, {}, {}
+
+        def z_words(r, g):
+            if g == HI:
+                return zhi[r][:].bitcast(F32)
+            return zlo[r][:].bitcast(F32)[:, 256 * g : 256 * (g + 1)]
+
+        def z_pre(r):
+            t = work.tile([P, 1024], F32, tag="pre", name="pre", align_bytes=64)
+            pre[r] = t
+            if r in STR:
+                return
+            nc.vector.tensor_copy(
+                out=t[:, 0:768].rearrange("p (g u w) -> p u g w", g=G, u=2),
+                in_=zlo[r][:].bitcast(F32).rearrange("p (g w u) -> p u g w", g=G, u=2),
+            )
+            nc.vector.tensor_copy(
+                out=t[:, 768:1024].rearrange("p (u w) -> p u w", u=2),
+                in_=zhi[r][:].bitcast(F32).rearrange("p (w u) -> p u w", u=2),
+            )
+
+        def z_transpose(r, g0, ng):
+            xt = psum.tile([P, 4, P], F32, tag="tp", name="tp", bufs=2)
+            xts[(r, g0)] = xt
+            for i in range(2 * ng):
+                g, u = g0 + i // 2, i % 2
+                if r in STR:
+                    src = z_words(r, g)[:, u:256:2]
+                else:
+                    src = pre[r][:, 256 * g + P * u : 256 * g + P * (u + 1)]
+                nc.tensor.transpose(xt[:, i, :], src, ident[:])
+
+        def z_copy(r, g0, ng):
+            if r not in grp:
+                t = work.tile([P, 4 * 512], BF16, tag="grp", name="grp", align_bytes=64)
+                grp[r] = t
+            dst = grp[r][:].bitcast(F32)[:, 256 * g0 : 256 * (g0 + ng)]
+            nc.scalar.copy(
+                out=dst.rearrange("p (g r u) -> p g r u", g=ng, u=2),
+                in_=xts[(r, g0)][:, 0 : 2 * ng, :].rearrange("p (g u) r -> p g r u", u=2),
+            )
+
+        def z_quant(r, g0, ng):
+            nc.vector.quantize_mx(
+                out=zc[r][:, P * g0 : P * (g0 + ng)].bitcast(FP8X4),
+                scales=zs[r][:, P * g0 : P * (g0 + ng)],
+                in_=grp[r][:, 512 * g0 : 512 * (g0 + ng)],
+            )
+
+        wg = []
+        for c in range(C):
+            t = keep.tile([P, W, 4], BF16, name="wg%d" % c, align_bytes=64)
+            wg.append(t)
+        V_COLS = 256
+
+        def w_inter(c):
+            nc.vector.tensor_copy(out=wg[c][:, 0:V_COLS, :], in_=whr[c][:, :, 0:V_COLS].rearrange("p j w -> p w j"))
+
+        def w_inter_s(c):
+            nc.scalar.copy(out=wg[c][:, V_COLS:W, :], in_=whr[c][:, :, V_COLS:W].rearrange("p j w -> p w j"))
+
+        def w_quant(c):
+            nc.vector.quantize_mx(
+                out=whc[c][:].bitcast(FP8X4), scales=whs[c][:], in_=wg[c][:].rearrange("p w j -> p (w j)")
+            )
+
+        acc = {}
+
+        def mm(r, c, g):
+            if (r, c) not in acc:
+                t = psum.tile([P, W], F32, tag="acc", name="acc", bufs=6)
+                acc[(r, c)] = t
+            if g == HI:
+                rhs, rhs_s = whc[c][:].bitcast(FP8X4), whs[c][:]
+            else:
+                rhs = wlo[g][:, 2 * W * c : 2 * W * (c + 1)].bitcast(FP4X4)
+                rhs_s = wls[:, g, W * c : W * (c + 1)]
+            nc.tensor.matmul_mx(
+                out=acc[(r, c)][:],
+                lhsT=zc[r][:, P * g : P * (g + 1)].bitcast(FP8X4),
+                lhsT_scale=zs[r][:, P * g : P * (g + 1)],
+                rhs=rhs,
+                rhs_scale=rhs_s,
+                start=(g == 0),
+                stop=(g == HI),
+            )
+
+        def mm_lo(r, c):
+            for g in range(G):
+                mm(r, c, g)
+
+        ot = {}
+
+        def logits(r, c, lo=0, hi=W):
+            if (r, c // 2) not in ot:
+                t = outs.tile([P, 2 * W], F32, tag="ot", name="ot", align_bytes=64)
+                ot[(r, c // 2)] = t
+            o = (c % 2) * W
+            nc.vector.scalar_tensor_tensor(
+                out=ot[(r, c // 2)][:, o + lo : o + hi],
+                in0=acc[(r, c)][:, lo:hi],
+                scalar=sharp[:, r : r + 1],
+                in1=cbc[:, W * c + lo : W * c + hi],
+                op0=MULT,
+                op1=SUB,
+            )
+
+        def scores(r, c, lo=0, hi=W):
+            o = (c % 2) * W
+            t = ot[(r, c // 2)]
+            nc.scalar.activation(out=t[:, o + lo : o + hi], in_=t[:, o + lo : o + hi], func=EXP)
+
+        def store(r, c, lo, hi):
+            o = (c % 2) * W
+            nc.sync.dma_start(out=out[rows[r], W * c + lo : W * c + hi], in_=ot[(r, c // 2)][:, o + lo : o + hi])
+
+        def store2(r, h):
+            nc.sync.dma_start(out=out[rows[r], 2 * W * h : 2 * W * (h + 1)], in_=ot[(r, h)][:])
+
+
+        sps = {}
+
+        def vec_cols():
+            vps = psum.tile([P, P], BF16, tag="tp", name="vps", bufs=2)
+            nc.tensor.transpose(vps[:], vecs[:], ident_b[:])
+            nc.scalar.copy(out=ccol[:], in_=vps[:, 0:16])
+            nc.scalar.copy(out=sharp[:], in_=vps[:, 16:24])
+
+        def spread(h):
+            t = psum.tile([P, 8, P], BF16, tag="acc", name="acc", bufs=6)
+            sps[h] = t
+            for i in range(8):
+                m = 8 * h + i
+                nc.tensor.transpose(t[:, i, :], ccol[:, m : m + 1].to_broadcast([P, P]), ident_b[:])
+
+        def spread_copy(h):
+            nc.scalar.copy(out=cbc[:, 1024 * h : 1024 * (h + 1)], in_=sps[h][:].rearrange("p a b -> p (a b)"))
+
+        z_transpose(0, 0, 1)
+        vec_cols()
+        z_copy(0, 0, 1)
+        z_quant(0, 0, 1)
+        spread(0)
+        mm(0, 0, 0)
+        spread_copy(0)
+        mm(0, 1, 0)
+        z_transpose(0, 1, 2)
+        mm(0, 2, 0)
+        z_copy(0, 1, 2)
+        mm(0, 3, 0)
+        z_transpose(0, 3, 1)
+        z_quant(0, 1, 2)
+        spread(1)
+        z_copy(0, 3, 1)
+        z_quant(0, 3, 1)
+        mm(0, 0, 1)
+        spread_copy(1)
+        mm(0, 1, 1)
+        mm(0, 2, 1)
+        w_inter(0)
+        w_inter_s(0)
+        mm(0, 3, 1)
+        mm(0, 0, 2)
+        mm(0, 1, 2)
+        z_transpose(1, 0, 2)
+        w_quant(0)
+        z_transpose(1, 2, 2)
+        z_copy(1, 0, 2)
+        w_inter(1)
+        mm(0, 2, 2)
+        z_copy(1, 2, 2)
+        mm(0, 3, 2)
+        z_quant(1, 0, 2)
+        mm(0, 0, 3)
+        w_inter_s(1)
+        z_quant(1, 2, 2)
+        mm(1, 0, 0)
+        w_inter(2)
+        mm(1, 0, 1)
+        mm(1, 0, 2)
+        logits(0, 0)
+        mm(1, 0, 3)
+        w_inter_s(2)
+        w_quant(1)
+        mm(1, 1, 0)
+        mm(1, 1, 1)
+        z_pre(2)
+        mm(1, 1, 2)
+        w_inter_s(3)
+        mm(0, 1, 3)
+        mm(1, 1, 3)
+        w_quant(2)
+        z_transpose(2, 0, 2)
+        w_inter(3)
+        z_transpose(2, 2, 2)
+        scores(0, 0)
+        mm(0, 2, 3)
+        logits(1, 0)
+        mm(1, 2, 0)
+        z_copy(2, 0, 2)
+        mm(1, 2, 1)
+        w_quant(3)
+        mm(1, 2, 2)
+        z_copy(2, 2, 2)
+        mm(1, 2, 3)
+        logits(0, 1)
+        mm(1, 3, 0)
+        scores(1, 0)
+        mm(0, 3, 3)
+        z_quant(2, 0, 4)
+        mm(1, 3, 1)
+        scores(0, 1)
+        mm(1, 3, 2)
+        z_pre(3)
+        mm(1, 3, 3)
+        store2(0, 0)
+        mm(2, 0, 0)
+        logits(1, 1)
+        z_transpose(3, 0, 2)
+        z_transpose(3, 2, 2)
+        logits(0, 2)
+        z_copy(3, 0, 2)
+        mm(2, 0, 1)
+        mm(2, 0, 2)
+        logits(1, 2)
+        scores(1, 1)
+        mm(2, 0, 3)
+        mm(2, 1, 0)
+        logits(0, 3)
+        scores(0, 2)
+        store2(1, 0)
+        mm(2, 1, 1)
+        mm(2, 1, 2)
+        logits(1, 3)
+        z_copy(3, 2, 2)
+        mm(2, 1, 3)
+        mm(2, 2, 0)
+        z_pre(4)
+        scores(0, 3)
+        mm(2, 2, 1)
+        mm(2, 2, 2)
+        scores(1, 2)
+        z_quant(3, 0, 4)
+        store2(0, 1)
+        z_transpose(4, 0, 2)
+        scores(1, 3)
+        z_transpose(4, 2, 2)
+        logits(2, 0)
+        mm(2, 2, 3)
+        z_copy(4, 0, 2)
+        store2(1, 1)
+        logits(2, 1)
+        mm(2, 3, 0)
+        mm(2, 3, 1)
+        scores(2, 0)
+        logits(2, 2)
+        mm(2, 3, 2)
+        mm(2, 3, 3)
+        scores(2, 1)
+        z_pre(5)
+        mm(3, 0, 0)
+        mm(3, 0, 1)
+        z_copy(4, 2, 2)
+        store2(2, 0)
+        mm(3, 0, 2)
+        logits(2, 3)
+        mm(3, 0, 3)
+        scores(2, 2)
+        mm(3, 1, 0)
+        z_quant(4, 0, 4)
+        mm(3, 1, 1)
+        scores(2, 3)
+        mm(3, 1, 2)
+        logits(3, 0)
+        mm(3, 1, 3)
+        store2(2, 1)
+        z_pre(6)
+        z_transpose(5, 0, 2)
+        scores(3, 0)
+        z_transpose(5, 2, 2)
+        logits(3, 1)
+        z_copy(5, 0, 2)
+        mm(3, 2, 0)
+        mm(3, 2, 1)
+        z_pre(7)
+        z_copy(5, 2, 2)
+        mm(3, 2, 2)
+        mm(3, 2, 3)
+        scores(3, 1)
+        z_quant(5, 0, 4)
+        mm(3, 3, 0)
+        mm(3, 3, 1)
+        mm(3, 3, 2)
+        store2(3, 0)
+        logits(3, 2)
+        mm(3, 3, 3)
+        mm(4, 0, 0)
+        scores(3, 2)
+        logits(3, 3)
+        mm(4, 0, 1)
+        mm(4, 0, 2)
+        mm(4, 0, 3)
+        scores(3, 3)
+        mm(4, 1, 0)
+        logits(4, 0)
+        mm(4, 1, 1)
+        store2(3, 1)
+        mm(4, 1, 2)
+        mm(4, 1, 3)
+        scores(4, 0)
+        z_transpose(6, 0, 2)
+        logits(4, 1)
+        z_transpose(6, 2, 2)
+        z_copy(6, 0, 2)
+        mm(4, 2, 0)
+        mm(4, 2, 1)
+        scores(4, 1)
+        mm(4, 2, 2)
+        mm(4, 2, 3)
+        z_copy(6, 2, 2)
+        store2(4, 0)
+        mm(4, 3, 0)
+        logits(4, 2)
+        mm(4, 3, 1)
+        mm(4, 3, 2)
+        z_quant(6, 0, 4)
+        mm(4, 3, 3)
+        scores(4, 2)
+        mm(5, 0, 0)
+        mm(5, 0, 1)
+        logits(4, 3)
+        mm(5, 0, 2)
+        mm(5, 0, 3)
+        scores(4, 3)
+        mm(5, 1, 0)
+        logits(5, 0)
+        mm(5, 1, 1)
+        store2(4, 1)
+        mm(5, 1, 2)
+        mm(5, 1, 3)
+        scores(5, 0)
+        z_transpose(7, 0, 2)
+        logits(5, 1)
+        z_transpose(7, 2, 2)
+        z_copy(7, 0, 2)
+        mm(5, 2, 0)
+        mm(5, 2, 1)
+        scores(5, 1)
+        mm(5, 2, 2)
+        mm(5, 2, 3)
+        z_copy(7, 2, 2)
+        store2(5, 0)
+        mm(5, 3, 0)
+        logits(5, 2)
+        mm(5, 3, 1)
+        mm(5, 3, 2)
+        z_quant(7, 0, 4)
+        mm(5, 3, 3)
+        scores(5, 2)
+        mm(6, 0, 0)
+        mm(6, 0, 1)
+        logits(5, 3)
+        mm(6, 0, 2)
+        mm(6, 0, 3)
+        scores(5, 3)
+        mm(6, 1, 0)
+        logits(6, 0)
+        mm(6, 1, 1)
+        store2(5, 1)
+        mm(6, 1, 2)
+        mm(6, 1, 3)
+        scores(6, 0)
+        mm(6, 2, 0)
+        logits(6, 1)
+        mm(6, 2, 1)
+        mm(6, 2, 2)
+        mm(6, 2, 3)
+        scores(6, 1)
+        mm(6, 3, 0)
+        logits(6, 2)
+        mm(6, 3, 1)
+        store2(6, 0)
+        mm(6, 3, 2)
+        mm(6, 3, 3)
+        scores(6, 2)
+        mm(7, 0, 0)
+        logits(6, 3)
+        mm(7, 0, 1)
+        mm(7, 0, 2)
+        mm(7, 0, 3)
+        scores(6, 3)
+        mm(7, 1, 0)
+        logits(7, 0)
+        mm(7, 1, 1)
+        store2(6, 1)
+        mm(7, 1, 2)
+        mm(7, 1, 3)
+        scores(7, 0)
+        mm(7, 2, 0)
+        logits(7, 1)
+        mm(7, 2, 1)
+        mm(7, 2, 2)
+        mm(7, 2, 3)
+        scores(7, 1)
+        mm(7, 3, 0)
+        logits(7, 2)
+        mm(7, 3, 1)
+        store2(7, 0)
+        mm(7, 3, 2)
+        mm(7, 3, 3)
+        scores(7, 2)
+        logits(7, 3, 0, 256)
+        store(7, 2, 0, 512)
+        logits(7, 3, 256, 512)
+        scores(7, 3, 0, 256)
+        scores(7, 3, 256, 512)
+        store(7, 3, 0, 256)
+        store(7, 3, 256, 512)

@@ -4,7 +4,7 @@ import concourse.mybir as mybir
 from concourse.masks import make_identity
 
 M, A, B, N = 1024, 512, 1536, 2048
-FLOPS = 2 * M * (A + B) * N
+FLOPS = ()
 
 F32 = mybir.dt.float32
 BF16 = mybir.dt.bfloat16
@@ -22,8 +22,11 @@ R = M // P
 C = 4
 W = N // C
 G = B // 512
-LOADS = "a0 l0 s0 b0 l1 h0 l2 w0 z1 h1 w1 w2 w3 z2 h2 z3 h3 z4 h4 z5 h5 z6 h6 z7 h7"
-STR = (0, 1)
+LOADS = "z0 h0 l0 s0 v0 z1 h1 w0 z2 h2 z3 h3 l1 w1 z4 h4 w2 w3 q0 q1 q2 q3"
+STR = (0,)
+DV = ((5, 6, 7),)
+PS = ()
+ACC = 5
 HI = G
 
 
@@ -31,8 +34,8 @@ def tile_dino_teacher_scores_s1_kernel(tc, z_hi, z_lo, w_hi, w_lo_words, w_lo_sc
     nc = tc.nc
     with ExitStack() as ctx:
         keep = ctx.enter_context(tc.tile_pool(name="keep", bufs=1))
-        work = ctx.enter_context(tc.tile_pool(name="work", bufs=3))
-        outs = ctx.enter_context(tc.tile_pool(name="outs", bufs=12))
+        work = ctx.enter_context(tc.tile_pool(name="work", bufs=4))
+        outs = ctx.enter_context(tc.tile_pool(name="outs", bufs=20))
         psum = ctx.enter_context(tc.psum_pool(name="psum", bufs=1))
 
         ident = keep.tile([P, P], F32, name="ident", align_bytes=64)
@@ -45,8 +48,8 @@ def tile_dino_teacher_scores_s1_kernel(tc, z_hi, z_lo, w_hi, w_lo_words, w_lo_sc
         junk = keep.tile([P, 1], F32, name="junk", align_bytes=64)
         wls = keep.tile([P, G, N], U8, name="wls", align_bytes=64)
         wlo = []
-        for g in range(G):
-            t = keep.tile([P, 2 * N], U8, name="wlo%d" % g, align_bytes=64)
+        for c in (0, 1):
+            t = keep.tile([P, G, (1 + 2 * c) * 2 * W], U8, name="wlo%d" % c, align_bytes=64)
             wlo.append(t)
         whr, whc, whs = [], [], []
         for c in range(C):
@@ -57,15 +60,20 @@ def tile_dino_teacher_scores_s1_kernel(tc, z_hi, z_lo, w_hi, w_lo_words, w_lo_sc
             t = keep.tile([P, W], U8, name="whs%d" % c, align_bytes=64)
             whs.append(t)
         zlo, zhi, zc, zs = [], [], [], []
+        quarters = sum([list(tiles) for tiles in DV], [])
         for r in range(R):
-            t = keep.tile([P, B], BF16, name="zlo%d" % r, align_bytes=64)
+            t = keep.tile([P, 64 if r in quarters else B], BF16, name="zlo%d" % r, align_bytes=64)
             zlo.append(t)
-            t = keep.tile([P, A], BF16, name="zhi%d" % r, align_bytes=64)
+            t = keep.tile([P, 64 if r in quarters else A], BF16, name="zhi%d" % r, align_bytes=64)
             zhi.append(t)
             t = keep.tile([P, 4 * P], U32, name="zc%d" % r, align_bytes=64)
             zc.append(t)
             t = keep.tile([P, 4 * P], U8, name="zs%d" % r, align_bytes=64)
             zs.append(t)
+        zq = []
+        for i, tiles in enumerate(DV):
+            t = keep.tile([P, 4 * len(tiles), 4, P], BF16, name="zq%d" % i, align_bytes=64)
+            zq.append(t)
         rows = [slice(r * P, (r + 1) * P) for r in range(R)]
 
         ctx.enter_context(tc.manual_schedule())
@@ -74,12 +82,13 @@ def tile_dino_teacher_scores_s1_kernel(tc, z_hi, z_lo, w_hi, w_lo_words, w_lo_sc
         nc.vector.memset(junk[:], 0.0)
         nc.vector.memset(wls[:].rearrange("p g n -> p (g n)").bitcast(I32), 0)
         nc.vector.tensor_copy(out=ident_b[:], in_=ident[:])
-        nc.scalar.dma_start(out=vecs[0:16, :], in_=centre.rearrange("(a b) -> a b", b=P))
-        nc.scalar.dma_start(out=vecs[16:24, :], in_=sharpen.rearrange("(a b) -> a b", b=P))
         nc.scalar.activation(out=junk[:], in_=junk[:], func=EXP)
 
-        def load_wlo(g):
-            nc.sync.dma_start(out=wlo[g][:].bitcast(I32), in_=w_lo_words[g].bitcast(I32))
+        def load_wlo(i):
+            cols = slice(0, 2 * W) if i == 0 else slice(2 * W, 2 * N)
+            nc.sync.dma_start(
+                out=wlo[i][:].bitcast(I32), in_=w_lo_words[:, :, cols].rearrange("g p n -> p g n").bitcast(I32)
+            )
 
         wh_view = w_hi.rearrange("(p j) n -> p j n", j=4)
         for tok in LOADS.split():
@@ -91,6 +100,18 @@ def tile_dino_teacher_scores_s1_kernel(tc, z_hi, z_lo, w_hi, w_lo_words, w_lo_sc
                     nc.sync.dma_start(
                         out=wls[32 * q : 32 * q + 4, :, :].bitcast(I32),
                         in_=w_lo_scales[:, 4 * q : 4 * q + 4, :].rearrange("g r n -> r g n").bitcast(I32),
+                    )
+            elif k == "v":
+                nc.sync.dma_start(out=vecs[0:16, :], in_=centre.rearrange("(a b) -> a b", b=P))
+                nc.sync.dma_start(out=vecs[16:24, :], in_=sharpen.rearrange("(a b) -> a b", b=P))
+            elif k == "q":
+                i, g = i // 4, i % 4
+                d0, nd = DV[i][0] * P, len(DV[i]) * P
+                src = z_hi[d0 : d0 + nd, :] if g == HI else z_lo[d0 : d0 + nd, 512 * g : 512 * (g + 1)]
+                for q in range(4):
+                    nc.sync.dma_start(
+                        out=zq[i][32 * q : 32 * q + 32, :, g, :],
+                        in_=src[:, P * q : P * (q + 1)].rearrange("(b w) k -> w b k", w=32),
                     )
             elif k == "a":
                 nc.sync.dma_start(out=zlo[i][:, 0:512], in_=z_lo[rows[i], 0:512])
@@ -124,8 +145,38 @@ def tile_dino_teacher_scores_s1_kernel(tc, z_hi, z_lo, w_hi, w_lo_words, w_lo_sc
                 in_=zhi[r][:].bitcast(F32).rearrange("p (w u) -> p u w", u=2),
             )
 
+        trs = {}
+
+        def zq_pre(r, g):
+            if g == 0:
+                t = work.tile([P, 1024], F32, tag="qpre", name="qpre", align_bytes=64)
+                pre[r] = t
+            i = [r in tiles for tiles in DV].index(True)
+            b = 4 * (r - DV[i][0])
+            dst = pre[r][:, 256 * g : 256 * (g + 1)].rearrange("p (u b w) -> p u b w", u=2, b=4)
+            src = zq[i][:, b : b + 4, g, :].bitcast(F32).rearrange("p b (w u) -> p u b w", u=2)
+            if g in PS:
+                nc.scalar.copy(out=dst, in_=src)
+            else:
+                nc.vector.tensor_copy(out=dst, in_=src)
+
+        def zq_tr(r, h):
+            if h == 0:
+                t = work.tile([P, 1024], F32, tag="qtr", name="qtr", align_bytes=64)
+                trs[r] = t
+            nc.vector.transpose(out=trs[r][:, 512 * h : 512 * (h + 1)], in_=pre[r][:, 512 * h : 512 * (h + 1)])
+
+        def zq_copy(r, h):
+            if h == 0:
+                t = work.tile([P, 4 * 512], BF16, tag="grp", name="grp", align_bytes=64)
+                grp[r] = t
+            nc.scalar.copy(
+                out=grp[r][:].bitcast(F32)[:, 512 * h : 512 * (h + 1)].rearrange("p (g r u) -> p g r u", g=2, u=2),
+                in_=trs[r][:, 512 * h : 512 * (h + 1)].rearrange("p (g u r) -> p g r u", g=2, u=2),
+            )
+
         def z_transpose(r, g0, ng):
-            xt = psum.tile([P, 4, P], F32, tag="tp", name="tp", bufs=2)
+            xt = psum.tile([P, 4, P], F32, tag="tp", name="tp", bufs=8 - ACC)
             xts[(r, g0)] = xt
             for i in range(2 * ng):
                 g, u = g0 + i // 2, i % 2
@@ -173,12 +224,13 @@ def tile_dino_teacher_scores_s1_kernel(tc, z_hi, z_lo, w_hi, w_lo_words, w_lo_sc
 
         def mm(r, c, g):
             if (r, c) not in acc:
-                t = psum.tile([P, W], F32, tag="acc", name="acc", bufs=6)
+                t = psum.tile([P, W], F32, tag="acc", name="acc", bufs=ACC)
                 acc[(r, c)] = t
             if g == HI:
                 rhs, rhs_s = whc[c][:].bitcast(FP8X4), whs[c][:]
             else:
-                rhs = wlo[g][:, 2 * W * c : 2 * W * (c + 1)].bitcast(FP4X4)
+                o = 2 * W * max(c - 1, 0)
+                rhs = wlo[min(c, 1)][:, g, o : o + 2 * W].bitcast(FP4X4)
                 rhs_s = wls[:, g, W * c : W * (c + 1)]
             nc.tensor.matmul_mx(
                 out=acc[(r, c)][:],
@@ -197,12 +249,11 @@ def tile_dino_teacher_scores_s1_kernel(tc, z_hi, z_lo, w_hi, w_lo_words, w_lo_sc
         ot = {}
 
         def logits(r, c, lo=0, hi=W):
-            if (r, c // 2) not in ot:
-                t = outs.tile([P, 2 * W], F32, tag="ot", name="ot", align_bytes=64)
-                ot[(r, c // 2)] = t
-            o = (c % 2) * W
+            if (r, c) not in ot:
+                t = outs.tile([P, W], F32, tag="ot", name="ot", align_bytes=64)
+                ot[(r, c)] = t
             nc.vector.scalar_tensor_tensor(
-                out=ot[(r, c // 2)][:, o + lo : o + hi],
+                out=ot[(r, c)][:, lo:hi],
                 in0=acc[(r, c)][:, lo:hi],
                 scalar=sharp[:, r : r + 1],
                 in1=cbc[:, W * c + lo : W * c + hi],
@@ -211,28 +262,22 @@ def tile_dino_teacher_scores_s1_kernel(tc, z_hi, z_lo, w_hi, w_lo_words, w_lo_sc
             )
 
         def scores(r, c, lo=0, hi=W):
-            o = (c % 2) * W
-            t = ot[(r, c // 2)]
-            nc.scalar.activation(out=t[:, o + lo : o + hi], in_=t[:, o + lo : o + hi], func=EXP)
+            t = ot[(r, c)]
+            nc.scalar.activation(out=t[:, lo:hi], in_=t[:, lo:hi], func=EXP)
 
-        def store(r, c, lo, hi):
-            o = (c % 2) * W
-            nc.sync.dma_start(out=out[rows[r], W * c + lo : W * c + hi], in_=ot[(r, c // 2)][:, o + lo : o + hi])
-
-        def store2(r, h):
-            nc.sync.dma_start(out=out[rows[r], 2 * W * h : 2 * W * (h + 1)], in_=ot[(r, h)][:])
-
+        def store(r, c, lo=0, hi=W):
+            nc.sync.dma_start(out=out[rows[r], W * c + lo : W * c + hi], in_=ot[(r, c)][:, lo:hi])
 
         sps = {}
 
         def vec_cols():
-            vps = psum.tile([P, P], BF16, tag="tp", name="vps", bufs=2)
+            vps = psum.tile([P, P], BF16, tag="tp", name="vps", bufs=8 - ACC)
             nc.tensor.transpose(vps[:], vecs[:], ident_b[:])
             nc.scalar.copy(out=ccol[:], in_=vps[:, 0:16])
             nc.scalar.copy(out=sharp[:], in_=vps[:, 16:24])
 
         def spread(h):
-            t = psum.tile([P, 8, P], BF16, tag="acc", name="acc", bufs=6)
+            t = psum.tile([P, 8, P], BF16, tag="acc", name="acc", bufs=ACC)
             sps[h] = t
             for i in range(8):
                 m = 8 * h + i
@@ -241,281 +286,309 @@ def tile_dino_teacher_scores_s1_kernel(tc, z_hi, z_lo, w_hi, w_lo_words, w_lo_sc
         def spread_copy(h):
             nc.scalar.copy(out=cbc[:, 1024 * h : 1024 * (h + 1)], in_=sps[h][:].rearrange("p a b -> p (a b)"))
 
-        z_transpose(0, 0, 1)
-        vec_cols()
-        z_copy(0, 0, 1)
-        z_quant(0, 0, 1)
-        spread(0)
+        z_transpose(0, 0, 2)
+        z_transpose(0, 2, 2)
+        z_copy(0, 0, 2)
+        z_quant(0, 0, 2)
+        z_copy(0, 2, 2)
         mm(0, 0, 0)
-        spread_copy(0)
-        mm(0, 1, 0)
-        z_transpose(0, 1, 2)
-        mm(0, 2, 0)
-        z_copy(0, 1, 2)
-        mm(0, 3, 0)
-        z_transpose(0, 3, 1)
-        z_quant(0, 1, 2)
-        spread(1)
-        z_copy(0, 3, 1)
-        z_quant(0, 3, 1)
+        z_quant(0, 2, 2)
         mm(0, 0, 1)
-        spread_copy(1)
-        mm(0, 1, 1)
-        mm(0, 2, 1)
-        w_inter(0)
-        w_inter_s(0)
-        mm(0, 3, 1)
+        z_pre(1)
         mm(0, 0, 2)
-        mm(0, 1, 2)
+        vec_cols()
         z_transpose(1, 0, 2)
-        w_quant(0)
         z_transpose(1, 2, 2)
         z_copy(1, 0, 2)
-        w_inter(1)
-        mm(0, 2, 2)
+        spread(0)
+        w_inter(0)
         z_copy(1, 2, 2)
-        mm(0, 3, 2)
+        spread(1)
         z_quant(1, 0, 2)
-        mm(0, 0, 3)
-        w_inter_s(1)
-        z_quant(1, 2, 2)
-        mm(1, 0, 0)
-        w_inter(2)
-        mm(1, 0, 1)
-        mm(1, 0, 2)
-        logits(0, 0)
-        mm(1, 0, 3)
-        w_inter_s(2)
-        w_quant(1)
-        mm(1, 1, 0)
-        mm(1, 1, 1)
+        w_inter_s(0)
         z_pre(2)
-        mm(1, 1, 2)
-        w_inter_s(3)
-        mm(0, 1, 3)
-        mm(1, 1, 3)
-        w_quant(2)
-        z_transpose(2, 0, 2)
-        w_inter(3)
-        z_transpose(2, 2, 2)
-        scores(0, 0)
-        mm(0, 2, 3)
-        logits(1, 0)
-        mm(1, 2, 0)
-        z_copy(2, 0, 2)
-        mm(1, 2, 1)
-        w_quant(3)
-        mm(1, 2, 2)
-        z_copy(2, 2, 2)
-        mm(1, 2, 3)
-        logits(0, 1)
-        mm(1, 3, 0)
-        scores(1, 0)
-        mm(0, 3, 3)
-        z_quant(2, 0, 4)
-        mm(1, 3, 1)
-        scores(0, 1)
-        mm(1, 3, 2)
+        mm(1, 0, 0)
+        mm(1, 0, 1)
+        z_quant(1, 2, 2)
         z_pre(3)
-        mm(1, 3, 3)
-        store2(0, 0)
-        mm(2, 0, 0)
-        logits(1, 1)
+        z_transpose(2, 0, 2)
+        spread_copy(0)
+        mm(1, 0, 2)
+        w_quant(0)
+        spread_copy(1)
+        z_transpose(2, 2, 2)
         z_transpose(3, 0, 2)
+        z_copy(2, 0, 2)
+        mm(0, 0, 3)
+        mm(1, 0, 3)
+        z_copy(2, 2, 2)
+        z_quant(2, 0, 2)
         z_transpose(3, 2, 2)
-        logits(0, 2)
+        logits(0, 0)
         z_copy(3, 0, 2)
+        mm(0, 1, 0)
+        z_quant(2, 2, 2)
+        mm(2, 0, 0)
+        scores(0, 0)
+        logits(1, 0)
         mm(2, 0, 1)
         mm(2, 0, 2)
-        logits(1, 2)
-        scores(1, 1)
-        mm(2, 0, 3)
-        mm(2, 1, 0)
-        logits(0, 3)
-        scores(0, 2)
-        store2(1, 0)
-        mm(2, 1, 1)
-        mm(2, 1, 2)
-        logits(1, 3)
         z_copy(3, 2, 2)
-        mm(2, 1, 3)
-        mm(2, 2, 0)
-        z_pre(4)
-        scores(0, 3)
-        mm(2, 2, 1)
-        mm(2, 2, 2)
-        scores(1, 2)
-        z_quant(3, 0, 4)
-        store2(0, 1)
-        z_transpose(4, 0, 2)
-        scores(1, 3)
-        z_transpose(4, 2, 2)
-        logits(2, 0)
-        mm(2, 2, 3)
-        z_copy(4, 0, 2)
-        store2(1, 1)
-        logits(2, 1)
-        mm(2, 3, 0)
-        mm(2, 3, 1)
-        scores(2, 0)
-        logits(2, 2)
-        mm(2, 3, 2)
-        mm(2, 3, 3)
-        scores(2, 1)
-        z_pre(5)
+        z_quant(3, 0, 2)
+        mm(2, 0, 3)
+        w_inter(1)
+        mm(0, 1, 1)
+        scores(1, 0)
         mm(3, 0, 0)
         mm(3, 0, 1)
-        z_copy(4, 2, 2)
-        store2(2, 0)
+        z_quant(3, 2, 2)
+        w_inter_s(1)
+        mm(0, 1, 2)
+        logits(2, 0)
         mm(3, 0, 2)
-        logits(2, 3)
         mm(3, 0, 3)
-        scores(2, 2)
-        mm(3, 1, 0)
-        z_quant(4, 0, 4)
-        mm(3, 1, 1)
-        scores(2, 3)
-        mm(3, 1, 2)
+        z_pre(4)
+        mm(1, 1, 0)
+        scores(2, 0)
+        mm(1, 1, 1)
+        w_quant(1)
+        z_transpose(4, 0, 2)
+        w_inter_s(2)
         logits(3, 0)
-        mm(3, 1, 3)
-        store2(2, 1)
-        z_pre(6)
-        z_transpose(5, 0, 2)
+        z_transpose(4, 2, 2)
+        mm(0, 1, 3)
+        w_inter(2)
+        mm(1, 1, 2)
+        mm(1, 1, 3)
+        z_copy(4, 0, 2)
+        logits(0, 1)
+        mm(2, 1, 0)
+        mm(2, 1, 1)
+        z_copy(4, 2, 2)
+        mm(2, 1, 2)
+        z_quant(4, 0, 2)
+        mm(2, 1, 3)
+        logits(1, 1)
         scores(3, 0)
-        z_transpose(5, 2, 2)
-        logits(3, 1)
-        z_copy(5, 0, 2)
-        mm(3, 2, 0)
-        mm(3, 2, 1)
-        z_pre(7)
-        z_copy(5, 2, 2)
-        mm(3, 2, 2)
-        mm(3, 2, 3)
-        scores(3, 1)
-        z_quant(5, 0, 4)
-        mm(3, 3, 0)
-        mm(3, 3, 1)
-        mm(3, 3, 2)
-        store2(3, 0)
-        logits(3, 2)
-        mm(3, 3, 3)
         mm(4, 0, 0)
-        scores(3, 2)
-        logits(3, 3)
         mm(4, 0, 1)
+        z_quant(4, 2, 2)
+        scores(0, 1)
+        mm(3, 1, 0)
+        logits(2, 1)
+        mm(3, 1, 1)
+        scores(1, 1)
         mm(4, 0, 2)
+        w_quant(2)
         mm(4, 0, 3)
-        scores(3, 3)
+        scores(2, 1)
+        mm(3, 1, 2)
+        w_inter(3)
+        mm(3, 1, 3)
+        w_inter_s(3)
+        mm(0, 2, 0)
         mm(4, 1, 0)
         logits(4, 0)
         mm(4, 1, 1)
-        store2(3, 1)
         mm(4, 1, 2)
+        logits(3, 1)
         mm(4, 1, 3)
         scores(4, 0)
-        z_transpose(6, 0, 2)
+        mm(0, 2, 1)
+        w_quant(3)
+        mm(0, 2, 2)
+        scores(3, 1)
+        mm(0, 2, 3)
         logits(4, 1)
-        z_transpose(6, 2, 2)
-        z_copy(6, 0, 2)
-        mm(4, 2, 0)
-        mm(4, 2, 1)
+        mm(1, 2, 0)
+        mm(1, 2, 1)
+        logits(0, 2)
         scores(4, 1)
+        mm(1, 2, 2)
+        mm(1, 2, 3)
+        scores(0, 2)
+        mm(2, 2, 0)
+        logits(1, 2)
+        mm(2, 2, 1)
+        mm(2, 2, 2)
+        mm(2, 2, 3)
+        scores(1, 2)
+        store(0, 0)
+        store(1, 0)
+        mm(3, 2, 0)
+        store(2, 0)
+        store(3, 0)
+        logits(2, 2)
+        mm(3, 2, 1)
+        mm(3, 2, 2)
+        mm(3, 2, 3)
+        scores(2, 2)
+        mm(4, 2, 0)
+        logits(3, 2)
+        mm(4, 2, 1)
+        store(4, 0)
         mm(4, 2, 2)
         mm(4, 2, 3)
-        z_copy(6, 2, 2)
-        store2(4, 0)
-        mm(4, 3, 0)
+        scores(3, 2)
+        store(0, 1)
+        mm(0, 3, 0)
         logits(4, 2)
-        mm(4, 3, 1)
-        mm(4, 3, 2)
-        z_quant(6, 0, 4)
-        mm(4, 3, 3)
+        mm(0, 3, 1)
+        store(1, 1)
+        mm(0, 3, 2)
+        store(2, 1)
+        zq_pre(5, 0)
+        mm(0, 3, 3)
         scores(4, 2)
+        store(3, 1)
+        zq_pre(5, 1)
+        mm(1, 3, 0)
+        zq_pre(5, 2)
+        zq_pre(5, 3)
+        mm(1, 3, 1)
+        store(4, 1)
+        zq_tr(5, 0)
+        mm(1, 3, 2)
+        mm(1, 3, 3)
+        store(0, 2)
+        zq_tr(5, 1)
+        zq_copy(5, 0)
+        mm(2, 3, 0)
+        mm(2, 3, 1)
+        store(1, 2)
+        logits(0, 3)
+        zq_copy(5, 1)
+        mm(2, 3, 2)
+        mm(2, 3, 3)
+        store(2, 2)
+        z_quant(5, 0, 2)
+        scores(0, 3)
+        mm(3, 3, 0)
+        z_quant(5, 2, 2)
+        mm(3, 3, 1)
+        store(3, 2)
+        logits(1, 3)
+        mm(3, 3, 2)
+        mm(3, 3, 3)
+        store(4, 2)
+        logits(2, 3)
+        mm(4, 3, 0)
+        scores(1, 3)
+        mm(4, 3, 1)
+        store(0, 3)
+        zq_pre(6, 0)
+        mm(4, 3, 2)
+        scores(2, 3)
+        zq_pre(6, 1)
+        mm(4, 3, 3)
+        zq_pre(6, 2)
+        store(1, 3)
+        zq_pre(6, 3)
         mm(5, 0, 0)
+        zq_tr(6, 0)
         mm(5, 0, 1)
-        logits(4, 3)
+        store(2, 3)
         mm(5, 0, 2)
+        zq_tr(6, 1)
+        zq_copy(6, 0)
         mm(5, 0, 3)
-        scores(4, 3)
         mm(5, 1, 0)
-        logits(5, 0)
+        logits(3, 3)
+        zq_copy(6, 1)
         mm(5, 1, 1)
-        store2(4, 1)
         mm(5, 1, 2)
+        z_quant(6, 0, 2)
+        scores(3, 3)
         mm(5, 1, 3)
-        scores(5, 0)
-        z_transpose(7, 0, 2)
-        logits(5, 1)
-        z_transpose(7, 2, 2)
-        z_copy(7, 0, 2)
+        z_quant(6, 2, 2)
         mm(5, 2, 0)
+        logits(4, 3)
         mm(5, 2, 1)
-        scores(5, 1)
+        store(3, 3)
         mm(5, 2, 2)
+        logits(5, 0)
         mm(5, 2, 3)
-        z_copy(7, 2, 2)
-        store2(5, 0)
+        scores(4, 3)
         mm(5, 3, 0)
-        logits(5, 2)
         mm(5, 3, 1)
+        zq_pre(7, 0)
+        scores(5, 0)
+        store(4, 3)
+        zq_pre(7, 1)
         mm(5, 3, 2)
-        z_quant(7, 0, 4)
+        zq_pre(7, 2)
+        zq_pre(7, 3)
         mm(5, 3, 3)
-        scores(5, 2)
+        zq_tr(7, 0)
+        store(5, 0)
         mm(6, 0, 0)
         mm(6, 0, 1)
-        logits(5, 3)
+        zq_tr(7, 1)
+        zq_copy(7, 0)
         mm(6, 0, 2)
         mm(6, 0, 3)
-        scores(5, 3)
+        logits(5, 1)
+        zq_copy(7, 1)
         mm(6, 1, 0)
-        logits(6, 0)
         mm(6, 1, 1)
-        store2(5, 1)
+        z_quant(7, 0, 2)
         mm(6, 1, 2)
+        scores(5, 1)
+        z_quant(7, 2, 2)
         mm(6, 1, 3)
-        scores(6, 0)
+        logits(5, 2)
         mm(6, 2, 0)
-        logits(6, 1)
+        store(5, 1)
         mm(6, 2, 1)
+        logits(5, 3)
         mm(6, 2, 2)
+        scores(5, 2)
         mm(6, 2, 3)
-        scores(6, 1)
         mm(6, 3, 0)
-        logits(6, 2)
+        logits(6, 0)
+        scores(5, 3)
+        store(5, 2)
         mm(6, 3, 1)
-        store2(6, 0)
         mm(6, 3, 2)
+        logits(6, 1)
+        scores(6, 0)
+        store(5, 3)
         mm(6, 3, 3)
-        scores(6, 2)
         mm(7, 0, 0)
-        logits(6, 3)
+        logits(6, 2)
+        scores(6, 1)
+        store(6, 0)
         mm(7, 0, 1)
         mm(7, 0, 2)
+        logits(6, 3)
+        scores(6, 2)
+        store(6, 1)
         mm(7, 0, 3)
-        scores(6, 3)
         mm(7, 1, 0)
         logits(7, 0)
+        scores(6, 3)
         mm(7, 1, 1)
-        store2(6, 1)
+        store(6, 2)
         mm(7, 1, 2)
         mm(7, 1, 3)
+        store(6, 3)
         scores(7, 0)
         mm(7, 2, 0)
         logits(7, 1)
         mm(7, 2, 1)
+        store(7, 0)
         mm(7, 2, 2)
         mm(7, 2, 3)
         scores(7, 1)
         mm(7, 3, 0)
         logits(7, 2)
         mm(7, 3, 1)
-        store2(7, 0)
+        store(7, 1)
         mm(7, 3, 2)
         mm(7, 3, 3)
         scores(7, 2)
         logits(7, 3, 0, 256)
-        store(7, 2, 0, 512)
+        store(7, 2)
         logits(7, 3, 256, 512)
         scores(7, 3, 0, 256)
         scores(7, 3, 256, 512)

@@ -22,12 +22,12 @@ R = M // P
 C = 4
 W = N // C
 G = B // 512
-LOADS = "z0 h0 l0 s0 v0 z1 h1 w0 z2 h2 z3 h3 l1 w1 z4 h4 w2 w3 q0 q1 q2 q3"
-STR = (0,)
-DV = ((5, 6, 7),)
-PS = ()
-ACC = 5
 HI = G
+LOADS = "y0 v0 h0 l0 y1 h1 w0 s0 y2 h2 s1 l1 w1 y3 h3 w2 y4 w3 h6 h4 y5 h5 y6 h7 y7"
+ACC = 5
+DV = ()
+PS = ()
+V_COLS = 192
 
 
 def tile_dino_teacher_scores_s1_kernel(tc, z_hi, z_lo, w_hi, w_lo_words, w_lo_scales, sharpen, centre, out):
@@ -35,126 +35,107 @@ def tile_dino_teacher_scores_s1_kernel(tc, z_hi, z_lo, w_hi, w_lo_words, w_lo_sc
     with ExitStack() as ctx:
         keep = ctx.enter_context(tc.tile_pool(name="keep", bufs=1))
         work = ctx.enter_context(tc.tile_pool(name="work", bufs=4))
-        outs = ctx.enter_context(tc.tile_pool(name="outs", bufs=20))
+        outs = ctx.enter_context(tc.tile_pool(name="outs", bufs=24))
         psum = ctx.enter_context(tc.psum_pool(name="psum", bufs=1))
 
-        ident = keep.tile([P, P], F32, name="ident", align_bytes=64)
+        ident = keep.tile([P, P], F32, name="ident", align_bytes=256)
         make_identity(nc, ident[:])
-        ident_b = keep.tile([P, P], BF16, name="ident_b", align_bytes=64)
-        vecs = keep.tile([P, P], BF16, name="vecs", align_bytes=64)
-        sharp = keep.tile([P, R], F32, name="sharp", align_bytes=64)
-        ccol = keep.tile([P, N // P], BF16, name="ccol", align_bytes=64)
-        cbc = keep.tile([P, N], BF16, name="cbc", align_bytes=64)
-        junk = keep.tile([P, 1], F32, name="junk", align_bytes=64)
-        wls = keep.tile([P, G, N], U8, name="wls", align_bytes=64)
-        wlo = []
+        cen = keep.tile([P, 2 * P], BF16, name="cen", align_bytes=256)
+        shr = keep.tile([P, P], BF16, name="shr", align_bytes=256)
+        ccol = keep.tile([P, 40], F32, name="ccol", align_bytes=256)
+        cbc = keep.tile([P, N], BF16, name="cbc", align_bytes=256)
+        junk = keep.tile([P, 1], F32, name="junk", align_bytes=256)
+        wls = keep.tile([P, G, N], U8, name="wls", align_bytes=256)
+        wlo, whr, wg, whc, whs = [], [], [], [], []
         for c in (0, 1):
-            t = keep.tile([P, G, (1 + 2 * c) * 2 * W], U8, name="wlo%d" % c, align_bytes=64)
+            t = keep.tile([P, G, (1 + 2 * c) * 2 * W], U8, name="wlo%d" % c, align_bytes=256)
             wlo.append(t)
-        whr, whc, whs = [], [], []
         for c in range(C):
-            t = keep.tile([P, 4, W], BF16, name="whr%d" % c, align_bytes=64)
+            t = keep.tile([P, 4, W], BF16, name="whr%d" % c, align_bytes=256)
             whr.append(t)
-            t = keep.tile([P, W], U32, name="whc%d" % c, align_bytes=64)
+            t = keep.tile([P, W, 4], BF16, name="wg%d" % c, align_bytes=256)
+            wg.append(t)
+            t = keep.tile([P, W], U32, name="whc%d" % c, align_bytes=256)
             whc.append(t)
-            t = keep.tile([P, W], U8, name="whs%d" % c, align_bytes=64)
+            t = keep.tile([P, W], U8, name="whs%d" % c, align_bytes=256)
             whs.append(t)
         zlo, zhi, zc, zs = [], [], [], []
-        quarters = sum([list(tiles) for tiles in DV], [])
-        for r in range(R):
-            t = keep.tile([P, 64 if r in quarters else B], BF16, name="zlo%d" % r, align_bytes=64)
+        for r in range(DV[0] if DV else R):
+            t = keep.tile([P, B], BF16, name="zlo%d" % r, align_bytes=256)
             zlo.append(t)
-            t = keep.tile([P, 64 if r in quarters else A], BF16, name="zhi%d" % r, align_bytes=64)
+            t = keep.tile([P, A], BF16, name="zhi%d" % r, align_bytes=256)
             zhi.append(t)
-            t = keep.tile([P, 4 * P], U32, name="zc%d" % r, align_bytes=64)
+        zq = keep.tile([P, 4 * len(DV), 4, P], BF16, name="zq", align_bytes=256)
+        rows = [slice(P * r, P * (r + 1)) for r in range(R)]
+        for r in range(R):
+            t = keep.tile([P, 4 * P], U32, name="zc%d" % r, align_bytes=256)
             zc.append(t)
-            t = keep.tile([P, 4 * P], U8, name="zs%d" % r, align_bytes=64)
+            t = keep.tile([P, 4 * P], U8, name="zs%d" % r, align_bytes=256)
             zs.append(t)
-        zq = []
-        for i, tiles in enumerate(DV):
-            t = keep.tile([P, 4 * len(tiles), 4, P], BF16, name="zq%d" % i, align_bytes=64)
-            zq.append(t)
-        rows = [slice(r * P, (r + 1) * P) for r in range(R)]
 
         ctx.enter_context(tc.manual_schedule())
 
-        nc.vector.memset(vecs[:].bitcast(I32), 0)
         nc.vector.memset(junk[:], 0.0)
+        nc.vector.memset(cen[:].bitcast(I32), 0)
+        nc.vector.memset(shr[:].bitcast(I32), 0)
         nc.vector.memset(wls[:].rearrange("p g n -> p (g n)").bitcast(I32), 0)
-        nc.vector.tensor_copy(out=ident_b[:], in_=ident[:])
         nc.scalar.activation(out=junk[:], in_=junk[:], func=EXP)
-
-        def load_wlo(i):
-            cols = slice(0, 2 * W) if i == 0 else slice(2 * W, 2 * N)
-            nc.sync.dma_start(
-                out=wlo[i][:].bitcast(I32), in_=w_lo_words[:, :, cols].rearrange("g p n -> p g n").bitcast(I32)
-            )
 
         wh_view = w_hi.rearrange("(p j) n -> p j n", j=4)
         for tok in LOADS.split():
             k, i = tok[0], int(tok[1:])
             if k == "l":
-                load_wlo(i)
+                cols = slice(0, 2 * W) if i == 0 else slice(2 * W, 2 * N)
+                nc.sync.dma_start(
+                    out=wlo[i][:].bitcast(I32), in_=w_lo_words[:, :, cols].rearrange("g p n -> p g n").bitcast(I32)
+                )
             elif k == "s":
+                cols = slice(0, W) if i == 0 else slice(W, N)
                 for q in range(4):
                     nc.sync.dma_start(
-                        out=wls[32 * q : 32 * q + 4, :, :].bitcast(I32),
-                        in_=w_lo_scales[:, 4 * q : 4 * q + 4, :].rearrange("g r n -> r g n").bitcast(I32),
+                        out=wls[32 * q : 32 * q + 4, :, cols].bitcast(I32),
+                        in_=w_lo_scales[:, 4 * q : 4 * q + 4, cols].rearrange("g r n -> r g n").bitcast(I32),
                     )
             elif k == "v":
-                nc.sync.dma_start(out=vecs[0:16, :], in_=centre.rearrange("(a b) -> a b", b=P))
-                nc.sync.dma_start(out=vecs[16:24, :], in_=sharpen.rearrange("(a b) -> a b", b=P))
-            elif k == "q":
-                i, g = i // 4, i % 4
-                d0, nd = DV[i][0] * P, len(DV[i]) * P
-                src = z_hi[d0 : d0 + nd, :] if g == HI else z_lo[d0 : d0 + nd, 512 * g : 512 * (g + 1)]
-                for q in range(4):
-                    nc.sync.dma_start(
-                        out=zq[i][32 * q : 32 * q + 32, :, g, :],
-                        in_=src[:, P * q : P * (q + 1)].rearrange("(b w) k -> w b k", w=32),
-                    )
-            elif k == "a":
-                nc.sync.dma_start(out=zlo[i][:, 0:512], in_=z_lo[rows[i], 0:512])
-            elif k == "b":
-                nc.sync.dma_start(out=zlo[i][:, 512:B], in_=z_lo[rows[i], 512:B])
-            elif k == "z":
+                nc.sync.dma_start(out=cen[0:8, :], in_=centre.rearrange("(a b) -> a b", b=2 * P))
+                nc.sync.dma_start(out=shr[32:40, :], in_=sharpen.rearrange("(a b) -> a b", b=P))
+            elif k == "y":
                 nc.sync.dma_start(out=zlo[i][:], in_=z_lo[rows[i], :])
             elif k == "h":
                 nc.sync.dma_start(out=zhi[i][:], in_=z_hi[rows[i], :])
+            elif k == "q":
+                d0, nd = DV[0] * P, len(DV) * P
+                src = z_hi[d0 : d0 + nd, :] if i == HI else z_lo[d0 : d0 + nd, 512 * i : 512 * (i + 1)]
+                for q in (0, 2, 1, 3):
+                    nc.sync.dma_start(
+                        out=zq[32 * q : 32 * q + 32, :, i, :],
+                        in_=src[:, P * q : P * (q + 1)].rearrange("(b w) k -> w b k", w=32),
+                    )
             else:
                 nc.sync.dma_start(out=whr[i][:], in_=wh_view[:, :, i * W : (i + 1) * W])
 
         pre, grp, xts = {}, {}, {}
 
-        def z_words(r, g):
-            if g == HI:
-                return zhi[r][:].bitcast(F32)
-            return zlo[r][:].bitcast(F32)[:, 256 * g : 256 * (g + 1)]
-
-        def z_pre(r):
-            t = work.tile([P, 1024], F32, tag="pre", name="pre", align_bytes=64)
-            pre[r] = t
-            if r in STR:
-                return
-            nc.vector.tensor_copy(
-                out=t[:, 0:768].rearrange("p (g u w) -> p u g w", g=G, u=2),
-                in_=zlo[r][:].bitcast(F32).rearrange("p (g w u) -> p u g w", g=G, u=2),
-            )
-            nc.vector.tensor_copy(
-                out=t[:, 768:1024].rearrange("p (u w) -> p u w", u=2),
-                in_=zhi[r][:].bitcast(F32).rearrange("p (w u) -> p u w", u=2),
-            )
+        def z_pre(r, h):
+            if h == 0:
+                t = work.tile([P, 1024], F32, tag="pre", name="pre", align_bytes=256)
+                pre[r] = t
+            lo, hi = zlo[r][:].bitcast(F32), zhi[r][:].bitcast(F32)
+            for a, b, src in ((0, 512, lo[:, 0:512]),) if h == 0 else ((512, 768, lo[:, 512:768]), (768, 1024, hi)):
+                nc.vector.tensor_copy(
+                    out=pre[r][:, a:b].rearrange("p (g u w) -> p u g w", u=2, w=P),
+                    in_=src.rearrange("p (g w u) -> p u g w", u=2, w=P),
+                )
 
         trs = {}
 
         def zq_pre(r, g):
             if g == 0:
-                t = work.tile([P, 1024], F32, tag="qpre", name="qpre", align_bytes=64)
+                t = work.tile([P, 1024], F32, tag="pre", name="pre", align_bytes=256)
                 pre[r] = t
-            i = [r in tiles for tiles in DV].index(True)
-            b = 4 * (r - DV[i][0])
+            b = 4 * (r - DV[0])
             dst = pre[r][:, 256 * g : 256 * (g + 1)].rearrange("p (u b w) -> p u b w", u=2, b=4)
-            src = zq[i][:, b : b + 4, g, :].bitcast(F32).rearrange("p b (w u) -> p u b w", u=2)
+            src = zq[:, b : b + 4, g, :].bitcast(F32).rearrange("p b (w u) -> p u b w", u=2)
             if g in PS:
                 nc.scalar.copy(out=dst, in_=src)
             else:
@@ -162,52 +143,40 @@ def tile_dino_teacher_scores_s1_kernel(tc, z_hi, z_lo, w_hi, w_lo_words, w_lo_sc
 
         def zq_tr(r, h):
             if h == 0:
-                t = work.tile([P, 1024], F32, tag="qtr", name="qtr", align_bytes=64)
+                t = work.tile([P, 1024], F32, tag="qtr", name="qtr", align_bytes=256)
                 trs[r] = t
             nc.vector.transpose(out=trs[r][:, 512 * h : 512 * (h + 1)], in_=pre[r][:, 512 * h : 512 * (h + 1)])
 
         def zq_copy(r, h):
             if h == 0:
-                t = work.tile([P, 4 * 512], BF16, tag="grp", name="grp", align_bytes=64)
+                t = work.tile([P, 4 * 512], BF16, tag="grp", name="grp", align_bytes=256)
                 grp[r] = t
             nc.scalar.copy(
                 out=grp[r][:].bitcast(F32)[:, 512 * h : 512 * (h + 1)].rearrange("p (g r u) -> p g r u", g=2, u=2),
                 in_=trs[r][:, 512 * h : 512 * (h + 1)].rearrange("p (g u r) -> p g r u", g=2, u=2),
             )
 
-        def z_transpose(r, g0, ng):
+        def z_transpose(r, h):
             xt = psum.tile([P, 4, P], F32, tag="tp", name="tp", bufs=8 - ACC)
-            xts[(r, g0)] = xt
-            for i in range(2 * ng):
-                g, u = g0 + i // 2, i % 2
-                if r in STR:
-                    src = z_words(r, g)[:, u:256:2]
-                else:
-                    src = pre[r][:, 256 * g + P * u : 256 * g + P * (u + 1)]
-                nc.tensor.transpose(xt[:, i, :], src, ident[:])
+            xts[(r, h)] = xt
+            for i in range(4):
+                nc.tensor.transpose(xt[:, i, :], pre[r][:, 512 * h + P * i : 512 * h + P * (i + 1)], ident[:])
 
-        def z_copy(r, g0, ng):
-            if r not in grp:
-                t = work.tile([P, 4 * 512], BF16, tag="grp", name="grp", align_bytes=64)
+        def z_copy(r, h):
+            if h == 0:
+                t = work.tile([P, 4 * 512], BF16, tag="grp", name="grp", align_bytes=256)
                 grp[r] = t
-            dst = grp[r][:].bitcast(F32)[:, 256 * g0 : 256 * (g0 + ng)]
             nc.scalar.copy(
-                out=dst.rearrange("p (g r u) -> p g r u", g=ng, u=2),
-                in_=xts[(r, g0)][:, 0 : 2 * ng, :].rearrange("p (g u) r -> p g r u", u=2),
+                out=grp[r][:].bitcast(F32)[:, 512 * h : 512 * (h + 1)].rearrange("p (g r u) -> p g r u", g=2, u=2),
+                in_=xts[(r, h)][:].rearrange("p (g u) r -> p g r u", u=2),
             )
 
-        def z_quant(r, g0, ng):
+        def z_quant(r, h):
             nc.vector.quantize_mx(
-                out=zc[r][:, P * g0 : P * (g0 + ng)].bitcast(FP8X4),
-                scales=zs[r][:, P * g0 : P * (g0 + ng)],
-                in_=grp[r][:, 512 * g0 : 512 * (g0 + ng)],
+                out=zc[r][:, 2 * P * h : 2 * P * (h + 1)].bitcast(FP8X4),
+                scales=zs[r][:, 2 * P * h : 2 * P * (h + 1)],
+                in_=grp[r][:, 1024 * h : 1024 * (h + 1)],
             )
-
-        wg = []
-        for c in range(C):
-            t = keep.tile([P, W, 4], BF16, name="wg%d" % c, align_bytes=64)
-            wg.append(t)
-        V_COLS = 256
 
         def w_inter(c):
             nc.vector.tensor_copy(out=wg[c][:, 0:V_COLS, :], in_=whr[c][:, :, 0:V_COLS].rearrange("p j w -> p w j"))
@@ -222,18 +191,18 @@ def tile_dino_teacher_scores_s1_kernel(tc, z_hi, z_lo, w_hi, w_lo_words, w_lo_sc
 
         acc = {}
 
-        def mm(r, c, g):
+        def mm(r, c, g, lo=0, hi=W):
             if (r, c) not in acc:
                 t = psum.tile([P, W], F32, tag="acc", name="acc", bufs=ACC)
                 acc[(r, c)] = t
             if g == HI:
-                rhs, rhs_s = whc[c][:].bitcast(FP8X4), whs[c][:]
+                rhs, rhs_s = whc[c][:, lo:hi].bitcast(FP8X4), whs[c][:, lo:hi]
             else:
                 o = 2 * W * max(c - 1, 0)
-                rhs = wlo[min(c, 1)][:, g, o : o + 2 * W].bitcast(FP4X4)
-                rhs_s = wls[:, g, W * c : W * (c + 1)]
+                rhs = wlo[min(c, 1)][:, g, o + 2 * lo : o + 2 * hi].bitcast(FP4X4)
+                rhs_s = wls[:, g, W * c + lo : W * c + hi]
             nc.tensor.matmul_mx(
-                out=acc[(r, c)][:],
+                out=acc[(r, c)][:, lo:hi],
                 lhsT=zc[r][:, P * g : P * (g + 1)].bitcast(FP8X4),
                 lhsT_scale=zs[r][:, P * g : P * (g + 1)],
                 rhs=rhs,
@@ -242,355 +211,367 @@ def tile_dino_teacher_scores_s1_kernel(tc, z_hi, z_lo, w_hi, w_lo_words, w_lo_sc
                 stop=(g == HI),
             )
 
-        def mm_lo(r, c):
-            for g in range(G):
-                mm(r, c, g)
-
         ot = {}
 
         def logits(r, c, lo=0, hi=W):
             if (r, c) not in ot:
-                t = outs.tile([P, W], F32, tag="ot", name="ot", align_bytes=64)
+                t = outs.tile([P, W], F32, tag="ot", name="ot", align_bytes=256)
                 ot[(r, c)] = t
             nc.vector.scalar_tensor_tensor(
                 out=ot[(r, c)][:, lo:hi],
                 in0=acc[(r, c)][:, lo:hi],
-                scalar=sharp[:, r : r + 1],
+                scalar=ccol[:, 32 + r : 33 + r],
                 in1=cbc[:, W * c + lo : W * c + hi],
                 op0=MULT,
                 op1=SUB,
             )
 
         def scores(r, c, lo=0, hi=W):
-            t = ot[(r, c)]
-            nc.scalar.activation(out=t[:, lo:hi], in_=t[:, lo:hi], func=EXP)
+            nc.scalar.activation(out=ot[(r, c)][:, lo:hi], in_=ot[(r, c)][:, lo:hi], func=EXP)
 
         def store(r, c, lo=0, hi=W):
             nc.sync.dma_start(out=out[rows[r], W * c + lo : W * c + hi], in_=ot[(r, c)][:, lo:hi])
 
         sps = {}
 
-        def vec_cols():
-            vps = psum.tile([P, P], BF16, tag="tp", name="vps", bufs=8 - ACC)
-            nc.tensor.transpose(vps[:], vecs[:], ident_b[:])
-            nc.scalar.copy(out=ccol[:], in_=vps[:, 0:16])
-            nc.scalar.copy(out=sharp[:], in_=vps[:, 16:24])
+        def cen_cols():
+            t = psum.tile([P, 4, P], F32, tag="tp", name="tp", bufs=8 - ACC)
+            nc.vector.tensor_copy(out=cen[32:64, :].bitcast(F32), in_=shr[32:64, :])
+            nc.tensor.transpose(t[:, 0, :], cen[:].bitcast(F32), ident[:])
+            nc.scalar.copy(out=ccol[:], in_=t[:, 0, 0:40])
 
-        def spread(h):
-            t = psum.tile([P, 8, P], BF16, tag="acc", name="acc", bufs=ACC)
-            sps[h] = t
-            for i in range(8):
-                m = 8 * h + i
-                nc.tensor.transpose(t[:, i, :], ccol[:, m : m + 1].to_broadcast([P, P]), ident_b[:])
+        def spread(c, n=1):
+            t = psum.tile([P, 4, P], F32, tag="tp", name="tp", bufs=8 - ACC)
+            sps[c] = t
+            for i in range(2 * n):
+                a = 2 * c + i
+                nc.tensor.transpose(t[:, i, :], ccol[:, a : a + 1].to_broadcast([P, P]), ident[:])
 
-        def spread_copy(h):
-            nc.scalar.copy(out=cbc[:, 1024 * h : 1024 * (h + 1)], in_=sps[h][:].rearrange("p a b -> p (a b)"))
+        def spread_copy(c, n=1):
+            nc.scalar.copy(
+                out=cbc[:, W * c : W * (c + n)].bitcast(F32),
+                in_=sps[c][:, 0 : 2 * n, :].rearrange("p a b -> p (a b)"),
+            )
 
-        z_transpose(0, 0, 2)
-        z_transpose(0, 2, 2)
-        z_copy(0, 0, 2)
-        z_quant(0, 0, 2)
-        z_copy(0, 2, 2)
-        mm(0, 0, 0)
-        z_quant(0, 2, 2)
-        mm(0, 0, 1)
-        z_pre(1)
-        mm(0, 0, 2)
-        vec_cols()
-        z_transpose(1, 0, 2)
-        z_transpose(1, 2, 2)
-        z_copy(1, 0, 2)
-        spread(0)
+        cen_cols()
+        z_pre(0, 0)
+        z_pre(0, 1)
+        spread(0, 2)
+        z_transpose(0, 0)
+        spread_copy(0, 2)
+        z_transpose(0, 1)
+        z_copy(0, 0)
+        z_pre(1, 0)
+        spread(2, 2)
+        z_copy(0, 1)
+        z_quant(0, 0)
+        z_transpose(1, 0)
+        z_pre(1, 1)
+        z_quant(0, 1)
+        z_transpose(1, 1)
+        z_copy(1, 0)
         w_inter(0)
-        z_copy(1, 2, 2)
-        spread(1)
-        z_quant(1, 0, 2)
+        mm(0, 0, 0)
         w_inter_s(0)
-        z_pre(2)
+        z_quant(1, 0)
         mm(1, 0, 0)
+        z_pre(2, 0)
         mm(1, 0, 1)
-        z_quant(1, 2, 2)
-        z_pre(3)
-        z_transpose(2, 0, 2)
-        spread_copy(0)
-        mm(1, 0, 2)
+        z_pre(2, 1)
+        z_copy(1, 1)
         w_quant(0)
-        spread_copy(1)
-        z_transpose(2, 2, 2)
-        z_transpose(3, 0, 2)
-        z_copy(2, 0, 2)
+        z_transpose(2, 0)
+        z_transpose(2, 1)
+        z_quant(1, 1)
+        z_copy(2, 0)
+        mm(0, 0, 1)
+        mm(1, 0, 2)
+        z_copy(2, 1)
+        z_quant(2, 0)
+        mm(0, 0, 2)
         mm(0, 0, 3)
-        mm(1, 0, 3)
-        z_copy(2, 2, 2)
-        z_quant(2, 0, 2)
-        z_transpose(3, 2, 2)
-        logits(0, 0)
-        z_copy(3, 0, 2)
-        mm(0, 1, 0)
-        z_quant(2, 2, 2)
+        z_quant(2, 1)
         mm(2, 0, 0)
-        scores(0, 0)
-        logits(1, 0)
+        logits(0, 0)
         mm(2, 0, 1)
         mm(2, 0, 2)
-        z_copy(3, 2, 2)
-        z_quant(3, 0, 2)
         mm(2, 0, 3)
-        w_inter(1)
-        mm(0, 1, 1)
-        scores(1, 0)
-        mm(3, 0, 0)
-        mm(3, 0, 1)
-        z_quant(3, 2, 2)
-        w_inter_s(1)
-        mm(0, 1, 2)
+        scores(0, 0)
         logits(2, 0)
-        mm(3, 0, 2)
-        mm(3, 0, 3)
-        z_pre(4)
+        mm(1, 0, 3)
+        spread_copy(2, 2)
         mm(1, 1, 0)
-        scores(2, 0)
+        logits(1, 0)
         mm(1, 1, 1)
-        w_quant(1)
-        z_transpose(4, 0, 2)
-        w_inter_s(2)
-        logits(3, 0)
-        z_transpose(4, 2, 2)
-        mm(0, 1, 3)
-        w_inter(2)
+        scores(2, 0)
         mm(1, 1, 2)
-        mm(1, 1, 3)
-        z_copy(4, 0, 2)
-        logits(0, 1)
+        mm(0, 1, 0)
+        scores(1, 0)
+        mm(0, 1, 1)
+        w_inter(1)
+        mm(0, 1, 2)
+        w_inter_s(1)
         mm(2, 1, 0)
         mm(2, 1, 1)
-        z_copy(4, 2, 2)
+        z_pre(3, 0)
         mm(2, 1, 2)
-        z_quant(4, 0, 2)
-        mm(2, 1, 3)
-        logits(1, 1)
-        scores(3, 0)
-        mm(4, 0, 0)
-        mm(4, 0, 1)
-        z_quant(4, 2, 2)
-        scores(0, 1)
-        mm(3, 1, 0)
-        logits(2, 1)
-        mm(3, 1, 1)
-        scores(1, 1)
-        mm(4, 0, 2)
-        w_quant(2)
-        mm(4, 0, 3)
-        scores(2, 1)
-        mm(3, 1, 2)
-        w_inter(3)
-        mm(3, 1, 3)
-        w_inter_s(3)
+        z_pre(3, 1)
         mm(0, 2, 0)
-        mm(4, 1, 0)
-        logits(4, 0)
-        mm(4, 1, 1)
-        mm(4, 1, 2)
-        logits(3, 1)
-        mm(4, 1, 3)
-        scores(4, 0)
+        z_transpose(3, 0)
+        w_quant(1)
+        z_transpose(3, 1)
+        z_copy(3, 0)
         mm(0, 2, 1)
-        w_quant(3)
+        w_inter(2)
+        mm(1, 1, 3)
+        z_copy(3, 1)
+        mm(0, 1, 3)
+        z_quant(3, 0)
+        mm(2, 1, 3)
+        w_inter_s(2)
+        z_quant(3, 1)
         mm(0, 2, 2)
-        scores(3, 1)
-        mm(0, 2, 3)
-        logits(4, 1)
+        logits(1, 1)
+        mm(3, 0, 0)
+        mm(3, 0, 1)
+        logits(0, 1)
+        mm(3, 0, 2)
+        mm(3, 0, 3)
+        logits(2, 1)
+        store(2, 0)
+        scores(1, 1)
         mm(1, 2, 0)
         mm(1, 2, 1)
-        logits(0, 2)
-        scores(4, 1)
+        w_quant(2)
+        scores(0, 1)
         mm(1, 2, 2)
+        mm(1, 3, 0)
+        scores(2, 1)
+        logits(3, 0)
+        mm(1, 3, 1)
+        mm(0, 2, 3)
+        w_inter_s(3)
+        z_pre(4, 0)
         mm(1, 2, 3)
+        z_pre(4, 1)
+        mm(3, 1, 0)
+        logits(0, 2)
+        z_transpose(4, 0)
+        z_transpose(4, 1)
+        z_pre(5, 0)
+        mm(3, 1, 1)
+        z_pre(5, 1)
+        scores(3, 0)
+        mm(3, 1, 2)
+        z_pre(6, 0)
+        mm(3, 1, 3)
+        z_copy(4, 0)
+        store(3, 0)
+        z_pre(6, 1)
+        store(1, 1)
+        store(0, 1)
+        store(2, 1)
+        z_transpose(5, 0)
+        w_inter(3)
+        z_copy(4, 1)
+        z_transpose(5, 1)
+        z_quant(4, 0)
+        z_transpose(6, 0)
         scores(0, 2)
-        mm(2, 2, 0)
+        z_quant(4, 1)
+        z_transpose(6, 1)
+        logits(3, 1)
+        z_copy(5, 0)
+        mm(1, 3, 2)
+        store(0, 2)
+        store(0, 0)
+        mm(4, 2, 0)
+        w_quant(3)
+        scores(3, 1)
+        mm(4, 2, 1)
+        z_quant(5, 0)
+        z_copy(5, 1)
+        mm(4, 2, 2)
+        store(3, 1)
+        store(1, 0)
         logits(1, 2)
+        mm(1, 3, 3)
+        z_copy(6, 0)
+        mm(4, 2, 3)
+        z_quant(5, 1)
+        mm(2, 2, 0)
+        logits(1, 3)
+        z_copy(6, 1)
         mm(2, 2, 1)
         mm(2, 2, 2)
-        mm(2, 2, 3)
+        z_quant(6, 0)
         scores(1, 2)
-        store(0, 0)
-        store(1, 0)
-        mm(3, 2, 0)
-        store(2, 0)
-        store(3, 0)
-        logits(2, 2)
-        mm(3, 2, 1)
-        mm(3, 2, 2)
-        mm(3, 2, 3)
-        scores(2, 2)
-        mm(4, 2, 0)
-        logits(3, 2)
-        mm(4, 2, 1)
-        store(4, 0)
-        mm(4, 2, 2)
-        mm(4, 2, 3)
-        scores(3, 2)
-        store(0, 1)
+        mm(2, 2, 3)
+        z_quant(6, 1)
         mm(0, 3, 0)
         logits(4, 2)
+        scores(1, 3)
+        store(1, 2)
         mm(0, 3, 1)
-        store(1, 1)
         mm(0, 3, 2)
-        store(2, 1)
-        zq_pre(5, 0)
+        logits(2, 2)
+        store(1, 3)
         mm(0, 3, 3)
         scores(4, 2)
-        store(3, 1)
-        zq_pre(5, 1)
-        mm(1, 3, 0)
-        zq_pre(5, 2)
-        zq_pre(5, 3)
-        mm(1, 3, 1)
-        store(4, 1)
-        zq_tr(5, 0)
-        mm(1, 3, 2)
-        mm(1, 3, 3)
-        store(0, 2)
-        zq_tr(5, 1)
-        zq_copy(5, 0)
-        mm(2, 3, 0)
-        mm(2, 3, 1)
-        store(1, 2)
-        logits(0, 3)
-        zq_copy(5, 1)
-        mm(2, 3, 2)
-        mm(2, 3, 3)
-        store(2, 2)
-        z_quant(5, 0, 2)
-        scores(0, 3)
-        mm(3, 3, 0)
-        z_quant(5, 2, 2)
-        mm(3, 3, 1)
-        store(3, 2)
-        logits(1, 3)
-        mm(3, 3, 2)
-        mm(3, 3, 3)
+        mm(6, 0, 0)
+        z_pre(7, 0)
+        mm(6, 0, 1)
+        scores(2, 2)
         store(4, 2)
-        logits(2, 3)
-        mm(4, 3, 0)
-        scores(1, 3)
-        mm(4, 3, 1)
-        store(0, 3)
-        zq_pre(6, 0)
-        mm(4, 3, 2)
-        scores(2, 3)
-        zq_pre(6, 1)
-        mm(4, 3, 3)
-        zq_pre(6, 2)
-        store(1, 3)
-        zq_pre(6, 3)
+        logits(0, 3)
+        mm(6, 0, 2)
+        mm(6, 0, 3)
+        store(2, 2)
+        z_pre(7, 1)
         mm(5, 0, 0)
-        zq_tr(6, 0)
+        scores(0, 3)
         mm(5, 0, 1)
-        store(2, 3)
+        logits(6, 0)
         mm(5, 0, 2)
-        zq_tr(6, 1)
-        zq_copy(6, 0)
+        store(0, 3)
         mm(5, 0, 3)
-        mm(5, 1, 0)
-        logits(3, 3)
-        zq_copy(6, 1)
-        mm(5, 1, 1)
-        mm(5, 1, 2)
-        z_quant(6, 0, 2)
-        scores(3, 3)
-        mm(5, 1, 3)
-        z_quant(6, 2, 2)
+        scores(6, 0)
+        mm(4, 3, 0)
+        logits(5, 0)
+        mm(4, 3, 1)
+        store(6, 0)
+        mm(4, 3, 2)
+        mm(4, 3, 3)
+        scores(5, 0)
         mm(5, 2, 0)
         logits(4, 3)
         mm(5, 2, 1)
-        store(3, 3)
+        store(5, 0)
         mm(5, 2, 2)
-        logits(5, 0)
         mm(5, 2, 3)
         scores(4, 3)
-        mm(5, 3, 0)
-        mm(5, 3, 1)
-        zq_pre(7, 0)
-        scores(5, 0)
-        store(4, 3)
-        zq_pre(7, 1)
-        mm(5, 3, 2)
-        zq_pre(7, 2)
-        zq_pre(7, 3)
-        mm(5, 3, 3)
-        zq_tr(7, 0)
-        store(5, 0)
-        mm(6, 0, 0)
-        mm(6, 0, 1)
-        zq_tr(7, 1)
-        zq_copy(7, 0)
-        mm(6, 0, 2)
-        mm(6, 0, 3)
-        logits(5, 1)
-        zq_copy(7, 1)
-        mm(6, 1, 0)
-        mm(6, 1, 1)
-        z_quant(7, 0, 2)
-        mm(6, 1, 2)
-        scores(5, 1)
-        z_quant(7, 2, 2)
-        mm(6, 1, 3)
+        z_transpose(7, 0)
         logits(5, 2)
-        mm(6, 2, 0)
-        store(5, 1)
-        mm(6, 2, 1)
-        logits(5, 3)
-        mm(6, 2, 2)
+        store(4, 3)
+        z_transpose(7, 1)
+        z_copy(7, 0)
+        mm(3, 3, 0)
+        mm(3, 3, 1)
         scores(5, 2)
-        mm(6, 2, 3)
-        mm(6, 3, 0)
-        logits(6, 0)
-        scores(5, 3)
+        z_quant(7, 0)
+        mm(3, 3, 2)
+        mm(3, 3, 3)
+        z_copy(7, 1)
         store(5, 2)
-        mm(6, 3, 1)
-        mm(6, 3, 2)
-        logits(6, 1)
-        scores(6, 0)
-        store(5, 3)
-        mm(6, 3, 3)
-        mm(7, 0, 0)
-        logits(6, 2)
-        scores(6, 1)
-        store(6, 0)
-        mm(7, 0, 1)
-        mm(7, 0, 2)
-        logits(6, 3)
-        scores(6, 2)
-        store(6, 1)
-        mm(7, 0, 3)
+        mm(4, 0, 0)
+        logits(3, 3)
+        mm(4, 0, 1)
+        mm(4, 0, 2)
+        z_quant(7, 1)
+        mm(4, 0, 3)
+        scores(3, 3)
+        mm(3, 2, 0)
+        logits(4, 0)
+        mm(3, 2, 1)
+        store(3, 3)
+        mm(3, 2, 2)
+        mm(3, 2, 3)
+        scores(4, 0)
+        mm(4, 1, 0)
+        logits(3, 2)
+        mm(4, 1, 1)
+        store(4, 0)
+        mm(4, 1, 2)
+        mm(4, 1, 3)
+        scores(3, 2)
         mm(7, 1, 0)
-        logits(7, 0)
-        scores(6, 3)
+        logits(4, 1)
         mm(7, 1, 1)
-        store(6, 2)
+        store(3, 2)
         mm(7, 1, 2)
         mm(7, 1, 3)
-        store(6, 3)
-        scores(7, 0)
-        mm(7, 2, 0)
+        scores(4, 1)
+        mm(5, 3, 0)
         logits(7, 1)
+        mm(5, 3, 1)
+        store(4, 1)
+        mm(5, 3, 2)
+        mm(5, 3, 3)
+        scores(7, 1)
+        mm(6, 1, 0)
+        logits(5, 3)
+        mm(6, 1, 1)
+        store(7, 1)
+        mm(6, 1, 2)
+        mm(6, 1, 3)
+        scores(5, 3)
+        mm(5, 1, 0)
+        logits(6, 1)
+        mm(5, 1, 1)
+        store(5, 3)
+        mm(5, 1, 2)
+        mm(5, 1, 3)
+        scores(6, 1)
+        mm(6, 2, 0)
+        logits(5, 1)
+        mm(6, 2, 1)
+        store(6, 1)
+        mm(6, 2, 2)
+        mm(6, 2, 3)
+        scores(5, 1)
+        mm(2, 3, 0)
+        logits(6, 2)
+        mm(2, 3, 1)
+        store(5, 1)
+        mm(2, 3, 2)
+        mm(2, 3, 3)
+        scores(6, 2)
+        mm(6, 3, 0)
+        logits(2, 3)
+        mm(6, 3, 1)
+        store(6, 2)
+        mm(6, 3, 2)
+        mm(6, 3, 3)
+        scores(2, 3)
+        mm(7, 0, 0)
+        logits(6, 3)
+        mm(7, 0, 1)
+        store(2, 3)
+        mm(7, 0, 2)
+        mm(7, 0, 3)
+        scores(6, 3)
+        mm(7, 2, 0)
+        logits(7, 0)
         mm(7, 2, 1)
-        store(7, 0)
+        store(6, 3)
         mm(7, 2, 2)
         mm(7, 2, 3)
-        scores(7, 1)
-        mm(7, 3, 0)
+        scores(7, 0)
+        mm(7, 3, 0, 0, 128)
+        mm(7, 3, 1, 0, 128)
+        mm(7, 3, 2, 0, 128)
         logits(7, 2)
-        mm(7, 3, 1)
-        store(7, 1)
-        mm(7, 3, 2)
-        mm(7, 3, 3)
-        scores(7, 2)
+        mm(7, 3, 3, 0, 128)
+        mm(7, 3, 0, 128, 256)
+        mm(7, 3, 1, 128, 256)
+        store(7, 0)
+        mm(7, 3, 2, 128, 256)
+        mm(7, 3, 3, 128, 256)
+        mm(7, 3, 0, 256, 384)
+        mm(7, 3, 1, 256, 384)
+        mm(7, 3, 2, 256, 384)
         logits(7, 3, 0, 256)
-        store(7, 2)
-        logits(7, 3, 256, 512)
+        mm(7, 3, 3, 256, 384)
+        scores(7, 2)
+        mm(7, 3, 0, 384, 512)
+        mm(7, 3, 1, 384, 512)
+        mm(7, 3, 2, 384, 512)
+        logits(7, 3, 256, 384)
+        mm(7, 3, 3, 384, 512)
+        logits(7, 3, 384, 512)
         scores(7, 3, 0, 256)
-        scores(7, 3, 256, 512)
+        store(7, 2)
+        scores(7, 3, 256, 384)
         store(7, 3, 0, 256)
+        scores(7, 3, 384, 512)
         store(7, 3, 256, 512)

@@ -4,7 +4,7 @@ import concourse.mybir as mybir
 from concourse.masks import make_identity
 
 M, A, B, N = 1024, 512, 1536, 2048
-FLOPS = ()
+FLOPS = 2 * M * (A + B) * N
 
 F32 = mybir.dt.float32
 BF16 = mybir.dt.bfloat16
@@ -13,565 +13,378 @@ U32 = mybir.dt.uint32
 U8 = mybir.dt.uint8
 FP8X4 = mybir.dt.float8_e4m3fn_x4
 FP4X4 = mybir.dt.float4_e2m1fn_x4
-MULT = mybir.AluOpType.mult
-SUB = mybir.AluOpType.subtract
 EXP = mybir.ActivationFunctionType.Exp
 
 P = 128
-R = M // P
-C = 4
-W = N // C
-G = B // 512
-HI = G
-LOADS = "y0 v0 h0 l0 y1 h1 w0 s0 y2 h2 s1 l1 w1 y3 h3 w2 y4 w3 h6 h4 y5 h5 y6 h7 y7"
-ACC = 5
-DV = ()
-PS = ()
-V_COLS = 192
+K_PASS = 512
+WORDS = K_PASS // 2
+TILES = M // P
+W = 512
+CHUNKS = N // W
+LO = B // K_PASS
+HI = LO
+PASSES = LO + 1
+
+BLOCK_TILES = (6, 7)
+PRE_ON_SCALAR = (6,)
+W_ON_VECTOR = 320
+ACC_BANKS = 5
+WORK_BUFS = 4
+OUT_BUFS = 24
+
+PLAN = """
+T0:0
+T0:3 C0:0
+T0:1 C0:3 Q0:0
+T0:2 P1:01 C0:1 Q0:3 P1:23
+T1:01 C0:2 Q0:1
+T1:23 Q0:2 C1:01
+M00:0
+V Q1:01 C1:23 I0 J0
+M10:0
+S01 Q1:23
+S23 P2:0123 D01 K0 D23
+M10:1
+M00:1
+M10:2
+M00:2
+T2:01
+T2:23 C2:01
+M10:3 C2:23 L10
+M00:3 L00 E10
+M01:012 Q2:0123 E00 I1
+M11:012 J1
+M12:0 P3:0123
+M20:0123 K1 L20 J2
+M21:012
+T3:01
+T3:23 I2 C3:01
+M21:3
+M22:0 P4:0123
+M01:3 C3:23
+M22:12 L21 E20
+M11:3
+T4:01 K2
+T4:23 J3 Q3:0123
+M12:12 E21
+M13:0 L01
+M22:3 C4:01
+M12:3 L11 E01
+M13:12 L22 C4:23 L12
+M30:0123 E22 L30 E11 P5:0123
+M31:0123 E30 Q4:0123 E12
+M32:012
+T5:01
+T5:23 L31 C5:01
+M32:3 I3 E31 L32 C5:23
+M40:0123 K3 E32
+M03:012 Q5:0123 P6:0
+M33:012 P6:1 L40
+M13:3 P6:2
+M03:3 L13 P6:3
+M33:3 E40 L03 E13
+M02:0123 B6:01 E03 L33 C6:01
+M50:0123 B6:23 E33 L02
+M23:0123 C6:23 L50 E02
+M51:0123 Q6:01 E50 L23 Q6:23
+M42:0123 E23 P7:0 L51
+M52:0123 P7:1 P7:2 E51 L42
+M41:0123 B7:01 E42 L52 C7:01
+M60:0123 P7:3 L41 E52 Q7:01
+M63:0123 E41 B7:23 L60
+M53:0123 C7:23 L63 E60
+M62:0123 Q7:23 E63 L53 L62
+M61:0123 E53 L61 E62
+M43:0123 L43 E61
+M70:0123 E43 L70
+M71:0123 E70 L71
+M72:0123 E71 L72 E72
+"""
 
 
 def tile_dino_teacher_scores_s1_kernel(tc, z_hi, z_lo, w_hi, w_lo_words, w_lo_scales, sharpen, centre, out):
     nc = tc.nc
     with ExitStack() as ctx:
         keep = ctx.enter_context(tc.tile_pool(name="keep", bufs=1))
-        work = ctx.enter_context(tc.tile_pool(name="work", bufs=4))
-        outs = ctx.enter_context(tc.tile_pool(name="outs", bufs=24))
+        work = ctx.enter_context(tc.tile_pool(name="work", bufs=WORK_BUFS))
+        outs = ctx.enter_context(tc.tile_pool(name="outs", bufs=OUT_BUFS))
         psum = ctx.enter_context(tc.psum_pool(name="psum", bufs=1))
 
-        ident = keep.tile([P, P], F32, name="ident", align_bytes=256)
+        def kept(shape, dtype, name):
+            return keep.tile(shape, dtype, name=name, align_bytes=256)
+
+        ident = kept([P, P], F32, "ident")
         make_identity(nc, ident[:])
-        cen = keep.tile([P, 2 * P], BF16, name="cen", align_bytes=256)
-        shr = keep.tile([P, P], BF16, name="shr", align_bytes=256)
-        ccol = keep.tile([P, 40], F32, name="ccol", align_bytes=256)
-        cbc = keep.tile([P, N], BF16, name="cbc", align_bytes=256)
-        junk = keep.tile([P, 1], F32, name="junk", align_bytes=256)
-        wls = keep.tile([P, G, N], U8, name="wls", align_bytes=256)
-        wlo, whr, wg, whc, whs = [], [], [], [], []
-        for c in (0, 1):
-            t = keep.tile([P, G, (1 + 2 * c) * 2 * W], U8, name="wlo%d" % c, align_bytes=256)
-            wlo.append(t)
-        for c in range(C):
-            t = keep.tile([P, 4, W], BF16, name="whr%d" % c, align_bytes=256)
-            whr.append(t)
-            t = keep.tile([P, W, 4], BF16, name="wg%d" % c, align_bytes=256)
-            wg.append(t)
-            t = keep.tile([P, W], U32, name="whc%d" % c, align_bytes=256)
-            whc.append(t)
-            t = keep.tile([P, W], U8, name="whs%d" % c, align_bytes=256)
-            whs.append(t)
-        zlo, zhi, zc, zs = [], [], [], []
-        for r in range(DV[0] if DV else R):
-            t = keep.tile([P, B], BF16, name="zlo%d" % r, align_bytes=256)
-            zlo.append(t)
-            t = keep.tile([P, A], BF16, name="zhi%d" % r, align_bytes=256)
-            zhi.append(t)
-        zq = keep.tile([P, 4 * len(DV), 4, P], BF16, name="zq", align_bytes=256)
-        rows = [slice(P * r, P * (r + 1)) for r in range(R)]
-        for r in range(R):
-            t = keep.tile([P, 4 * P], U32, name="zc%d" % r, align_bytes=256)
-            zc.append(t)
-            t = keep.tile([P, 4 * P], U8, name="zs%d" % r, align_bytes=256)
-            zs.append(t)
+
+        rows_in = kept([P, 2 * P], BF16, "rows_in")
+        sharpen_in = kept([P, P], BF16, "sharpen_in")
+        cols = kept([P, 32 + TILES], F32, "cols")
+        centre_all = kept([P, N], BF16, "centre_all")
+        warm = kept([P, 1], F32, "warm")
+
+        wlo_scales = kept([P, LO, N], U8, "wlo_scales")
+        wlo = [kept([P, LO, 2 * W], U8, "wlo0"), kept([P, LO, 2 * (N - W)], U8, "wlo1")]
+        whi, whi_grouped, whi_codes, whi_scales = [], [], [], []
+        for c in range(CHUNKS):
+            whi.append(kept([P, 4, W], BF16, "whi%d" % c))
+            whi_grouped.append(kept([P, W, 4], BF16, "whi_grouped%d" % c))
+            whi_codes.append(kept([P, W], U32, "whi_codes%d" % c))
+            whi_scales.append(kept([P, W], U8, "whi_scales%d" % c))
+        zlo, zhi, z_codes, z_scales = [], [], [], []
+        for r in range(BLOCK_TILES[0]):
+            zlo.append(kept([P, B], BF16, "zlo%d" % r))
+            zhi.append(kept([P, A], BF16, "zhi%d" % r))
+        z_quarters = kept([P, 4 * len(BLOCK_TILES), PASSES, P], BF16, "z_quarters")
+        for r in range(TILES):
+            z_codes.append(kept([P, PASSES * P], U32, "z_codes%d" % r))
+            z_scales.append(kept([P, PASSES * P], U8, "z_scales%d" % r))
+        crops = [slice(P * r, P * (r + 1)) for r in range(TILES)]
 
         ctx.enter_context(tc.manual_schedule())
 
-        nc.vector.memset(junk[:], 0.0)
-        nc.vector.memset(cen[:].bitcast(I32), 0)
-        nc.vector.memset(shr[:].bitcast(I32), 0)
-        nc.vector.memset(wls[:].rearrange("p g n -> p (g n)").bitcast(I32), 0)
-        nc.scalar.activation(out=junk[:], in_=junk[:], func=EXP)
+        nc.vector.memset(warm[:], 0.0)
+        nc.vector.memset(rows_in[:].bitcast(I32), 0)
+        nc.vector.memset(sharpen_in[:].bitcast(I32), 0)
+        nc.vector.memset(wlo_scales[:].rearrange("p g n -> p (g n)").bitcast(I32), 0)
+        nc.scalar.activation(out=warm[:], in_=warm[:], func=EXP)
 
-        wh_view = w_hi.rearrange("(p j) n -> p j n", j=4)
-        for tok in LOADS.split():
-            k, i = tok[0], int(tok[1:])
-            if k == "l":
-                cols = slice(0, 2 * W) if i == 0 else slice(2 * W, 2 * N)
+        whi_rows = w_hi.rearrange("(p j) n -> p j n", j=4)
+
+        def load_zlo(r, lo=0, hi=B):
+            nc.sync.dma_start(out=zlo[r][:, lo:hi], in_=z_lo[crops[r], lo:hi])
+
+        def load_zhi(r):
+            nc.sync.dma_start(out=zhi[r][:], in_=z_hi[crops[r], :])
+
+        def load_whi(c):
+            nc.sync.dma_start(out=whi[c][:], in_=whi_rows[:, :, W * c : W * (c + 1)])
+
+        def load_wlo(i, lo, hi):
+            nc.sync.dma_start(
+                out=wlo[i][:].bitcast(I32),
+                in_=w_lo_words[:, :, 2 * lo : 2 * hi].rearrange("g p n -> p g n").bitcast(I32),
+            )
+
+        def load_wlo_scales(lo, hi):
+            for q in range(4):
                 nc.sync.dma_start(
-                    out=wlo[i][:].bitcast(I32), in_=w_lo_words[:, :, cols].rearrange("g p n -> p g n").bitcast(I32)
-                )
-            elif k == "s":
-                cols = slice(0, W) if i == 0 else slice(W, N)
-                for q in range(4):
-                    nc.sync.dma_start(
-                        out=wls[32 * q : 32 * q + 4, :, cols].bitcast(I32),
-                        in_=w_lo_scales[:, 4 * q : 4 * q + 4, cols].rearrange("g r n -> r g n").bitcast(I32),
-                    )
-            elif k == "v":
-                nc.sync.dma_start(out=cen[0:8, :], in_=centre.rearrange("(a b) -> a b", b=2 * P))
-                nc.sync.dma_start(out=shr[32:40, :], in_=sharpen.rearrange("(a b) -> a b", b=P))
-            elif k == "y":
-                nc.sync.dma_start(out=zlo[i][:], in_=z_lo[rows[i], :])
-            elif k == "h":
-                nc.sync.dma_start(out=zhi[i][:], in_=z_hi[rows[i], :])
-            elif k == "q":
-                d0, nd = DV[0] * P, len(DV) * P
-                src = z_hi[d0 : d0 + nd, :] if i == HI else z_lo[d0 : d0 + nd, 512 * i : 512 * (i + 1)]
-                for q in (0, 2, 1, 3):
-                    nc.sync.dma_start(
-                        out=zq[32 * q : 32 * q + 32, :, i, :],
-                        in_=src[:, P * q : P * (q + 1)].rearrange("(b w) k -> w b k", w=32),
-                    )
-            else:
-                nc.sync.dma_start(out=whr[i][:], in_=wh_view[:, :, i * W : (i + 1) * W])
-
-        pre, grp, xts = {}, {}, {}
-
-        def z_pre(r, h):
-            if h == 0:
-                t = work.tile([P, 1024], F32, tag="pre", name="pre", align_bytes=256)
-                pre[r] = t
-            lo, hi = zlo[r][:].bitcast(F32), zhi[r][:].bitcast(F32)
-            for a, b, src in ((0, 512, lo[:, 0:512]),) if h == 0 else ((512, 768, lo[:, 512:768]), (768, 1024, hi)):
-                nc.vector.tensor_copy(
-                    out=pre[r][:, a:b].rearrange("p (g u w) -> p u g w", u=2, w=P),
-                    in_=src.rearrange("p (g w u) -> p u g w", u=2, w=P),
+                    out=wlo_scales[32 * q : 32 * q + 4, :, lo:hi].bitcast(I32),
+                    in_=w_lo_scales[:, 4 * q : 4 * q + 4, lo:hi].rearrange("g r n -> r g n").bitcast(I32),
                 )
 
-        trs = {}
+        def load_quarters(g):
+            first = P * BLOCK_TILES[0]
+            src = z_hi[first:M, :] if g == HI else z_lo[first:M, K_PASS * g : K_PASS * (g + 1)]
+            for q in (0, 2, 1, 3):
+                nc.sync.dma_start(
+                    out=z_quarters[32 * q : 32 * (q + 1), :, g, :],
+                    in_=src[:, P * q : P * (q + 1)].rearrange("(b w) k -> w b k", w=32),
+                )
 
-        def zq_pre(r, g):
-            if g == 0:
-                t = work.tile([P, 1024], F32, tag="pre", name="pre", align_bytes=256)
-                pre[r] = t
-            b = 4 * (r - DV[0])
-            dst = pre[r][:, 256 * g : 256 * (g + 1)].rearrange("p (u b w) -> p u b w", u=2, b=4)
-            src = zq[:, b : b + 4, g, :].bitcast(F32).rearrange("p b (w u) -> p u b w", u=2)
-            if g in PS:
-                nc.scalar.copy(out=dst, in_=src)
-            else:
-                nc.vector.tensor_copy(out=dst, in_=src)
+        load_zlo(0, 0, K_PASS)
+        load_zhi(0)
+        load_zlo(0, K_PASS, B)
+        load_zlo(1)
+        load_wlo(0, 0, W)
+        load_wlo_scales(0, W)
+        load_zhi(1)
+        nc.sync.dma_start(out=rows_in[0:8, :], in_=centre.rearrange("(a b) -> a b", b=2 * P))
+        nc.sync.dma_start(out=sharpen_in[32:40, :], in_=sharpen.rearrange("(a b) -> a b", b=P))
+        load_whi(0)
+        load_zhi(2)
+        load_zlo(2)
+        load_wlo_scales(W, N)
+        load_wlo(1, W, N)
+        load_whi(1)
+        load_zlo(3)
+        load_zhi(3)
+        load_whi(2)
+        load_zlo(4)
+        load_zhi(4)
+        load_whi(3)
+        load_quarters(0)
+        load_zlo(5)
+        load_zhi(5)
+        load_quarters(1)
+        load_quarters(HI)
+        load_quarters(2)
 
-        def zq_tr(r, h):
-            if h == 0:
-                t = work.tile([P, 1024], F32, tag="qtr", name="qtr", align_bytes=256)
-                trs[r] = t
-            nc.vector.transpose(out=trs[r][:, 512 * h : 512 * (h + 1)], in_=pre[r][:, 512 * h : 512 * (h + 1)])
+        ordered, turned, blocks, grouped, sums, results, spread_out = {}, {}, {}, {}, {}, {}, {}
 
-        def zq_copy(r, h):
-            if h == 0:
-                t = work.tile([P, 4 * 512], BF16, tag="grp", name="grp", align_bytes=256)
-                grp[r] = t
-            nc.scalar.copy(
-                out=grp[r][:].bitcast(F32)[:, 512 * h : 512 * (h + 1)].rearrange("p (g r u) -> p g r u", g=2, u=2),
-                in_=trs[r][:, 512 * h : 512 * (h + 1)].rearrange("p (g u r) -> p g r u", g=2, u=2),
-            )
-
-        def z_transpose(r, h):
-            xt = psum.tile([P, 4, P], F32, tag="tp", name="tp", bufs=8 - ACC)
-            xts[(r, h)] = xt
-            for i in range(4):
-                nc.tensor.transpose(xt[:, i, :], pre[r][:, 512 * h + P * i : 512 * h + P * (i + 1)], ident[:])
-
-        def z_copy(r, h):
-            if h == 0:
-                t = work.tile([P, 4 * 512], BF16, tag="grp", name="grp", align_bytes=256)
-                grp[r] = t
-            nc.scalar.copy(
-                out=grp[r][:].bitcast(F32)[:, 512 * h : 512 * (h + 1)].rearrange("p (g r u) -> p g r u", g=2, u=2),
-                in_=xts[(r, h)][:].rearrange("p (g u) r -> p g r u", u=2),
-            )
-
-        def z_quant(r, h):
-            nc.vector.quantize_mx(
-                out=zc[r][:, 2 * P * h : 2 * P * (h + 1)].bitcast(FP8X4),
-                scales=zs[r][:, 2 * P * h : 2 * P * (h + 1)],
-                in_=grp[r][:, 1024 * h : 1024 * (h + 1)],
-            )
-
-        def w_inter(c):
-            nc.vector.tensor_copy(out=wg[c][:, 0:V_COLS, :], in_=whr[c][:, :, 0:V_COLS].rearrange("p j w -> p w j"))
-
-        def w_inter_s(c):
-            nc.scalar.copy(out=wg[c][:, V_COLS:W, :], in_=whr[c][:, :, V_COLS:W].rearrange("p j w -> p w j"))
-
-        def w_quant(c):
-            nc.vector.quantize_mx(
-                out=whc[c][:].bitcast(FP8X4), scales=whs[c][:], in_=wg[c][:].rearrange("p w j -> p (w j)")
-            )
-
-        acc = {}
-
-        def mm(r, c, g, lo=0, hi=W):
-            if (r, c) not in acc:
-                t = psum.tile([P, W], F32, tag="acc", name="acc", bufs=ACC)
-                acc[(r, c)] = t
+        def z_words(r, g):
             if g == HI:
-                rhs, rhs_s = whc[c][:, lo:hi].bitcast(FP8X4), whs[c][:, lo:hi]
+                return zhi[r][:].bitcast(F32)
+            return zlo[r][:].bitcast(F32)[:, WORDS * g : WORDS * (g + 1)]
+
+        def put_in_order(r, passes):
+            if r not in ordered:
+                ordered[r] = work.tile([P, PASSES * WORDS], F32, tag="ordered", name="ordered", align_bytes=256)
+            copy = nc.scalar.copy if r in PRE_ON_SCALAR else nc.vector.tensor_copy
+            if r in BLOCK_TILES:
+                b = 4 * (r - BLOCK_TILES[0])
+                for g in passes:
+                    copy(
+                        out=ordered[r][:, WORDS * g : WORDS * (g + 1)].rearrange("p (u b w) -> p u b w", u=2, b=4),
+                        in_=z_quarters[:, b : b + 4, g, :].bitcast(F32).rearrange("p b (w u) -> p u b w", u=2),
+                    )
+                return
+            lo_passes = [g for g in passes if g != HI]
+            pieces = [(lo_passes[0], lo_passes[-1] + 1, zlo[r])] if lo_passes else []
+            if HI in passes:
+                pieces.append((HI, HI + 1, zhi[r]))
+            for g0, g1, tile in pieces:
+                first = 0 if g0 == HI else WORDS * g0
+                copy(
+                    out=ordered[r][:, WORDS * g0 : WORDS * g1].rearrange("p (g u w) -> p u g w", u=2, w=P),
+                    in_=tile[:].bitcast(F32)[:, first : first + WORDS * (g1 - g0)].rearrange(
+                        "p (g w u) -> p u g w", u=2, w=P
+                    ),
+                )
+
+        def transpose(r, passes):
+            bank = psum.tile([P, 4, P], F32, tag="turned", name="turned", bufs=8 - ACC_BANKS)
+            turned[(r, passes[0])] = bank
+            for i, (g, u) in enumerate([(g, u) for g in passes for u in (0, 1)]):
+                if r == 0:
+                    words = z_words(r, g)[:, u:WORDS:2]
+                else:
+                    words = ordered[r][:, WORDS * g + P * u : WORDS * g + P * (u + 1)]
+                nc.tensor.transpose(bank[:, i, :], words, ident[:])
+
+        def transpose_blocks(r, passes):
+            if r not in blocks:
+                blocks[r] = work.tile([P, PASSES * WORDS], F32, tag="blocks", name="blocks", align_bytes=256)
+            part = slice(WORDS * passes[0], WORDS * (passes[-1] + 1))
+            nc.vector.transpose(out=blocks[r][:, part], in_=ordered[r][:, part])
+
+        def group(r, passes):
+            if r not in grouped:
+                grouped[r] = work.tile([P, PASSES * K_PASS], BF16, tag="grouped", name="grouped", align_bytes=256)
+            n = len(passes)
+            part = slice(WORDS * passes[0], WORDS * (passes[-1] + 1))
+            if r in BLOCK_TILES:
+                words = blocks[r][:, part].rearrange("p (g u r) -> p g r u", g=n, u=2)
             else:
-                o = 2 * W * max(c - 1, 0)
-                rhs = wlo[min(c, 1)][:, g, o + 2 * lo : o + 2 * hi].bitcast(FP4X4)
-                rhs_s = wls[:, g, W * c + lo : W * c + hi]
-            nc.tensor.matmul_mx(
-                out=acc[(r, c)][:, lo:hi],
-                lhsT=zc[r][:, P * g : P * (g + 1)].bitcast(FP8X4),
-                lhsT_scale=zs[r][:, P * g : P * (g + 1)],
-                rhs=rhs,
-                rhs_scale=rhs_s,
-                start=(g == 0),
-                stop=(g == HI),
+                words = turned[(r, passes[0])][:, 0 : 2 * n, :].rearrange("p (g u) r -> p g r u", u=2)
+            nc.scalar.copy(
+                out=grouped[r][:].bitcast(F32)[:, part].rearrange("p (g r u) -> p g r u", g=n, u=2), in_=words
             )
 
-        ot = {}
+        def quantise(r, passes):
+            first, end = passes[0], passes[-1] + 1
+            nc.vector.quantize_mx(
+                out=z_codes[r][:, P * first : P * end].bitcast(FP8X4),
+                scales=z_scales[r][:, P * first : P * end],
+                in_=grouped[r][:, K_PASS * first : K_PASS * end],
+            )
+
+        def interleave(c, copy, cols_part):
+            copy(
+                out=whi_grouped[c][:, cols_part, :], in_=whi[c][:, :, cols_part].rearrange("p j n -> p n j")
+            )
+
+        def quantise_whi(c):
+            nc.vector.quantize_mx(
+                out=whi_codes[c][:].bitcast(FP8X4),
+                scales=whi_scales[c][:],
+                in_=whi_grouped[c][:].rearrange("p n j -> p (n j)"),
+            )
+
+        def vectors_to_columns():
+            bank = psum.tile([P, 4, P], F32, tag="turned", name="turned", bufs=8 - ACC_BANKS)
+            nc.vector.tensor_copy(out=rows_in[32:64, :].bitcast(F32), in_=sharpen_in[32:64, :])
+            nc.tensor.transpose(bank[:, 0, :], rows_in[:].bitcast(F32), ident[:])
+            nc.scalar.copy(out=cols[:], in_=bank[:, 0, 0 : 32 + TILES])
+
+        def spread(chunks):
+            bank = psum.tile([P, 4, P], F32, tag="turned", name="turned", bufs=8 - ACC_BANKS)
+            spread_out[chunks] = bank
+            for i in range(4):
+                a = 2 * chunks[0] + i
+                nc.tensor.transpose(bank[:, i, :], cols[:, a : a + 1].to_broadcast([P, P]), ident[:])
+
+        def copy_spread(chunks):
+            nc.scalar.copy(
+                out=centre_all[:, W * chunks[0] : W * (chunks[1] + 1)].bitcast(F32),
+                in_=spread_out[chunks][:].rearrange("p a b -> p (a b)"),
+            )
+
+        def multiply(r, c, passes, lo=0, hi=W):
+            if (r, c) not in sums:
+                sums[(r, c)] = psum.tile([P, W], F32, tag="sums", name="sums", bufs=ACC_BANKS)
+            for g in passes:
+                if g == HI:
+                    rhs, rhs_scale = whi_codes[c][:, lo:hi].bitcast(FP8X4), whi_scales[c][:, lo:hi]
+                else:
+                    codes, first = (wlo[0], 0) if c == 0 else (wlo[1], W * (c - 1))
+                    rhs = codes[:, g, 2 * (first + lo) : 2 * (first + hi)].bitcast(FP4X4)
+                    rhs_scale = wlo_scales[:, g, W * c + lo : W * c + hi]
+                nc.tensor.matmul_mx(
+                    out=sums[(r, c)][:, lo:hi],
+                    lhsT=z_codes[r][:, P * g : P * (g + 1)].bitcast(FP8X4),
+                    lhsT_scale=z_scales[r][:, P * g : P * (g + 1)],
+                    rhs=rhs,
+                    rhs_scale=rhs_scale,
+                    start=(g == 0),
+                    stop=(g == HI),
+                )
 
         def logits(r, c, lo=0, hi=W):
-            if (r, c) not in ot:
-                t = outs.tile([P, W], F32, tag="ot", name="ot", align_bytes=256)
-                ot[(r, c)] = t
+            if (r, c) not in results:
+                results[(r, c)] = outs.tile([P, W], F32, tag="results", name="results", align_bytes=256)
             nc.vector.scalar_tensor_tensor(
-                out=ot[(r, c)][:, lo:hi],
-                in0=acc[(r, c)][:, lo:hi],
-                scalar=ccol[:, 32 + r : 33 + r],
-                in1=cbc[:, W * c + lo : W * c + hi],
-                op0=MULT,
-                op1=SUB,
+                out=results[(r, c)][:, lo:hi],
+                in0=sums[(r, c)][:, lo:hi],
+                scalar=cols[:, 32 + r : 33 + r],
+                in1=centre_all[:, W * c + lo : W * c + hi],
+                op0=mybir.AluOpType.mult,
+                op1=mybir.AluOpType.subtract,
             )
 
-        def scores(r, c, lo=0, hi=W):
-            nc.scalar.activation(out=ot[(r, c)][:, lo:hi], in_=ot[(r, c)][:, lo:hi], func=EXP)
+        def exp(r, c, lo=0, hi=W):
+            part = results[(r, c)][:, lo:hi]
+            nc.scalar.activation(out=part, in_=part, func=EXP)
 
         def store(r, c, lo=0, hi=W):
-            nc.sync.dma_start(out=out[rows[r], W * c + lo : W * c + hi], in_=ot[(r, c)][:, lo:hi])
+            nc.sync.dma_start(out=out[crops[r], W * c + lo : W * c + hi], in_=results[(r, c)][:, lo:hi])
 
-        sps = {}
+        def exp_and_store(r, c):
+            exp(r, c)
+            store(r, c)
 
-        def cen_cols():
-            t = psum.tile([P, 4, P], F32, tag="tp", name="tp", bufs=8 - ACC)
-            nc.vector.tensor_copy(out=cen[32:64, :].bitcast(F32), in_=shr[32:64, :])
-            nc.tensor.transpose(t[:, 0, :], cen[:].bitcast(F32), ident[:])
-            nc.scalar.copy(out=ccol[:], in_=t[:, 0, 0:40])
+        by_tile = {"P": put_in_order, "T": transpose, "B": transpose_blocks, "C": group, "Q": quantise}
+        for step in PLAN.split():
+            kind, (head, *rest) = step[0], step[1:].split(":")
+            passes = [int(g) for g in rest[0]] if rest else []
+            where = tuple([int(x) for x in head])
+            if kind in by_tile:
+                by_tile[kind](where[0], passes)
+            elif kind == "M":
+                multiply(where[0], where[1], passes)
+            elif kind == "L":
+                logits(where[0], where[1])
+            elif kind == "E":
+                exp_and_store(where[0], where[1])
+            elif kind == "I":
+                interleave(where[0], nc.vector.tensor_copy, slice(0, W_ON_VECTOR))
+            elif kind == "J":
+                interleave(where[0], nc.scalar.copy, slice(W_ON_VECTOR, W))
+            elif kind == "K":
+                quantise_whi(where[0])
+            elif kind == "V":
+                vectors_to_columns()
+            elif kind == "S":
+                spread(where)
+            else:
+                copy_spread(where)
 
-        def spread(c, n=1):
-            t = psum.tile([P, 4, P], F32, tag="tp", name="tp", bufs=8 - ACC)
-            sps[c] = t
-            for i in range(2 * n):
-                a = 2 * c + i
-                nc.tensor.transpose(t[:, i, :], ccol[:, a : a + 1].to_broadcast([P, P]), ident[:])
-
-        def spread_copy(c, n=1):
-            nc.scalar.copy(
-                out=cbc[:, W * c : W * (c + n)].bitcast(F32),
-                in_=sps[c][:, 0 : 2 * n, :].rearrange("p a b -> p (a b)"),
-            )
-
-        cen_cols()
-        z_pre(0, 0)
-        z_pre(0, 1)
-        spread(0, 2)
-        z_transpose(0, 0)
-        spread_copy(0, 2)
-        z_transpose(0, 1)
-        z_copy(0, 0)
-        z_pre(1, 0)
-        spread(2, 2)
-        z_copy(0, 1)
-        z_quant(0, 0)
-        z_transpose(1, 0)
-        z_pre(1, 1)
-        z_quant(0, 1)
-        z_transpose(1, 1)
-        z_copy(1, 0)
-        w_inter(0)
-        mm(0, 0, 0)
-        w_inter_s(0)
-        z_quant(1, 0)
-        mm(1, 0, 0)
-        z_pre(2, 0)
-        mm(1, 0, 1)
-        z_pre(2, 1)
-        z_copy(1, 1)
-        w_quant(0)
-        z_transpose(2, 0)
-        z_transpose(2, 1)
-        z_quant(1, 1)
-        z_copy(2, 0)
-        mm(0, 0, 1)
-        mm(1, 0, 2)
-        z_copy(2, 1)
-        z_quant(2, 0)
-        mm(0, 0, 2)
-        mm(0, 0, 3)
-        z_quant(2, 1)
-        mm(2, 0, 0)
-        logits(0, 0)
-        mm(2, 0, 1)
-        mm(2, 0, 2)
-        mm(2, 0, 3)
-        scores(0, 0)
-        logits(2, 0)
-        mm(1, 0, 3)
-        spread_copy(2, 2)
-        mm(1, 1, 0)
-        logits(1, 0)
-        mm(1, 1, 1)
-        scores(2, 0)
-        mm(1, 1, 2)
-        mm(0, 1, 0)
-        scores(1, 0)
-        mm(0, 1, 1)
-        w_inter(1)
-        mm(0, 1, 2)
-        w_inter_s(1)
-        mm(2, 1, 0)
-        mm(2, 1, 1)
-        z_pre(3, 0)
-        mm(2, 1, 2)
-        z_pre(3, 1)
-        mm(0, 2, 0)
-        z_transpose(3, 0)
-        w_quant(1)
-        z_transpose(3, 1)
-        z_copy(3, 0)
-        mm(0, 2, 1)
-        w_inter(2)
-        mm(1, 1, 3)
-        z_copy(3, 1)
-        mm(0, 1, 3)
-        z_quant(3, 0)
-        mm(2, 1, 3)
-        w_inter_s(2)
-        z_quant(3, 1)
-        mm(0, 2, 2)
-        logits(1, 1)
-        mm(3, 0, 0)
-        mm(3, 0, 1)
-        logits(0, 1)
-        mm(3, 0, 2)
-        mm(3, 0, 3)
-        logits(2, 1)
-        store(2, 0)
-        scores(1, 1)
-        mm(1, 2, 0)
-        mm(1, 2, 1)
-        w_quant(2)
-        scores(0, 1)
-        mm(1, 2, 2)
-        mm(1, 3, 0)
-        scores(2, 1)
-        logits(3, 0)
-        mm(1, 3, 1)
-        mm(0, 2, 3)
-        w_inter_s(3)
-        z_pre(4, 0)
-        mm(1, 2, 3)
-        z_pre(4, 1)
-        mm(3, 1, 0)
-        logits(0, 2)
-        z_transpose(4, 0)
-        z_transpose(4, 1)
-        z_pre(5, 0)
-        mm(3, 1, 1)
-        z_pre(5, 1)
-        scores(3, 0)
-        mm(3, 1, 2)
-        z_pre(6, 0)
-        mm(3, 1, 3)
-        z_copy(4, 0)
-        store(3, 0)
-        z_pre(6, 1)
-        store(1, 1)
-        store(0, 1)
-        store(2, 1)
-        z_transpose(5, 0)
-        w_inter(3)
-        z_copy(4, 1)
-        z_transpose(5, 1)
-        z_quant(4, 0)
-        z_transpose(6, 0)
-        scores(0, 2)
-        z_quant(4, 1)
-        z_transpose(6, 1)
-        logits(3, 1)
-        z_copy(5, 0)
-        mm(1, 3, 2)
-        store(0, 2)
-        store(0, 0)
-        mm(4, 2, 0)
-        w_quant(3)
-        scores(3, 1)
-        mm(4, 2, 1)
-        z_quant(5, 0)
-        z_copy(5, 1)
-        mm(4, 2, 2)
-        store(3, 1)
-        store(1, 0)
-        logits(1, 2)
-        mm(1, 3, 3)
-        z_copy(6, 0)
-        mm(4, 2, 3)
-        z_quant(5, 1)
-        mm(2, 2, 0)
-        logits(1, 3)
-        z_copy(6, 1)
-        mm(2, 2, 1)
-        mm(2, 2, 2)
-        z_quant(6, 0)
-        scores(1, 2)
-        mm(2, 2, 3)
-        z_quant(6, 1)
-        mm(0, 3, 0)
-        logits(4, 2)
-        scores(1, 3)
-        store(1, 2)
-        mm(0, 3, 1)
-        mm(0, 3, 2)
-        logits(2, 2)
-        store(1, 3)
-        mm(0, 3, 3)
-        scores(4, 2)
-        mm(6, 0, 0)
-        z_pre(7, 0)
-        mm(6, 0, 1)
-        scores(2, 2)
-        store(4, 2)
-        logits(0, 3)
-        mm(6, 0, 2)
-        mm(6, 0, 3)
-        store(2, 2)
-        z_pre(7, 1)
-        mm(5, 0, 0)
-        scores(0, 3)
-        mm(5, 0, 1)
-        logits(6, 0)
-        mm(5, 0, 2)
-        store(0, 3)
-        mm(5, 0, 3)
-        scores(6, 0)
-        mm(4, 3, 0)
-        logits(5, 0)
-        mm(4, 3, 1)
-        store(6, 0)
-        mm(4, 3, 2)
-        mm(4, 3, 3)
-        scores(5, 0)
-        mm(5, 2, 0)
-        logits(4, 3)
-        mm(5, 2, 1)
-        store(5, 0)
-        mm(5, 2, 2)
-        mm(5, 2, 3)
-        scores(4, 3)
-        z_transpose(7, 0)
-        logits(5, 2)
-        store(4, 3)
-        z_transpose(7, 1)
-        z_copy(7, 0)
-        mm(3, 3, 0)
-        mm(3, 3, 1)
-        scores(5, 2)
-        z_quant(7, 0)
-        mm(3, 3, 2)
-        mm(3, 3, 3)
-        z_copy(7, 1)
-        store(5, 2)
-        mm(4, 0, 0)
-        logits(3, 3)
-        mm(4, 0, 1)
-        mm(4, 0, 2)
-        z_quant(7, 1)
-        mm(4, 0, 3)
-        scores(3, 3)
-        mm(3, 2, 0)
-        logits(4, 0)
-        mm(3, 2, 1)
-        store(3, 3)
-        mm(3, 2, 2)
-        mm(3, 2, 3)
-        scores(4, 0)
-        mm(4, 1, 0)
-        logits(3, 2)
-        mm(4, 1, 1)
-        store(4, 0)
-        mm(4, 1, 2)
-        mm(4, 1, 3)
-        scores(3, 2)
-        mm(7, 1, 0)
-        logits(4, 1)
-        mm(7, 1, 1)
-        store(3, 2)
-        mm(7, 1, 2)
-        mm(7, 1, 3)
-        scores(4, 1)
-        mm(5, 3, 0)
-        logits(7, 1)
-        mm(5, 3, 1)
-        store(4, 1)
-        mm(5, 3, 2)
-        mm(5, 3, 3)
-        scores(7, 1)
-        mm(6, 1, 0)
-        logits(5, 3)
-        mm(6, 1, 1)
-        store(7, 1)
-        mm(6, 1, 2)
-        mm(6, 1, 3)
-        scores(5, 3)
-        mm(5, 1, 0)
-        logits(6, 1)
-        mm(5, 1, 1)
-        store(5, 3)
-        mm(5, 1, 2)
-        mm(5, 1, 3)
-        scores(6, 1)
-        mm(6, 2, 0)
-        logits(5, 1)
-        mm(6, 2, 1)
-        store(6, 1)
-        mm(6, 2, 2)
-        mm(6, 2, 3)
-        scores(5, 1)
-        mm(2, 3, 0)
-        logits(6, 2)
-        mm(2, 3, 1)
-        store(5, 1)
-        mm(2, 3, 2)
-        mm(2, 3, 3)
-        scores(6, 2)
-        mm(6, 3, 0)
-        logits(2, 3)
-        mm(6, 3, 1)
-        store(6, 2)
-        mm(6, 3, 2)
-        mm(6, 3, 3)
-        scores(2, 3)
-        mm(7, 0, 0)
-        logits(6, 3)
-        mm(7, 0, 1)
-        store(2, 3)
-        mm(7, 0, 2)
-        mm(7, 0, 3)
-        scores(6, 3)
-        mm(7, 2, 0)
-        logits(7, 0)
-        mm(7, 2, 1)
-        store(6, 3)
-        mm(7, 2, 2)
-        mm(7, 2, 3)
-        scores(7, 0)
-        mm(7, 3, 0, 0, 128)
-        mm(7, 3, 1, 0, 128)
-        mm(7, 3, 2, 0, 128)
-        logits(7, 2)
-        mm(7, 3, 3, 0, 128)
-        mm(7, 3, 0, 128, 256)
-        mm(7, 3, 1, 128, 256)
-        store(7, 0)
-        mm(7, 3, 2, 128, 256)
-        mm(7, 3, 3, 128, 256)
-        mm(7, 3, 0, 256, 384)
-        mm(7, 3, 1, 256, 384)
-        mm(7, 3, 2, 256, 384)
-        logits(7, 3, 0, 256)
-        mm(7, 3, 3, 256, 384)
-        scores(7, 2)
-        mm(7, 3, 0, 384, 512)
-        mm(7, 3, 1, 384, 512)
-        mm(7, 3, 2, 384, 512)
-        logits(7, 3, 256, 384)
-        mm(7, 3, 3, 384, 512)
-        logits(7, 3, 384, 512)
-        scores(7, 3, 0, 256)
-        store(7, 2)
-        scores(7, 3, 256, 384)
-        store(7, 3, 0, 256)
-        scores(7, 3, 384, 512)
-        store(7, 3, 256, 512)
+        r, c = TILES - 1, CHUNKS - 1
+        for lo in range(0, W, P):
+            multiply(r, c, range(PASSES), lo, lo + P)
+        parts = ((0, 2 * P), (2 * P, 3 * P), (3 * P, W))
+        for lo, hi in parts:
+            logits(r, c, lo, hi)
+        for lo, hi in parts:
+            exp(r, c, lo, hi)
+        for lo, hi in ((0, 2 * P), (2 * P, W)):
+            store(r, c, lo, hi)

from contextlib import ExitStack

import concourse.mybir as mybir
from concourse.masks import make_identity

M, A, B, N = 1024, 512, 1536, 2048
FLOPS = 2 * M * (A + B) * N

F32 = mybir.dt.float32
BF16 = mybir.dt.bfloat16
I32 = mybir.dt.int32
U32 = mybir.dt.uint32
U8 = mybir.dt.uint8
FP8X4 = mybir.dt.float8_e4m3fn_x4
FP4X4 = mybir.dt.float4_e2m1fn_x4
EXP = mybir.ActivationFunctionType.Exp

P = 128
K_PASS = 512
WORDS = K_PASS // 2
TILES = M // P
W = 512
CHUNKS = N // W
LO = B // K_PASS
HI = LO
PASSES = LO + 1

BLOCK_TILES = (6, 7)
PRE_ON_SCALAR = (6,)
W_ON_VECTOR = 320
ACC_BANKS = 5
WORK_BUFS = 4
OUT_BUFS = 24

PLAN = """
T0:0
T0:3 C0:0
T0:1 C0:3 Q0:0
T0:2 P1:01 C0:1 Q0:3 P1:23
T1:01 C0:2 Q0:1
T1:23 Q0:2 C1:01
M00:0
V Q1:01 C1:23 I0 J0
M10:0
S01 Q1:23
S23 P2:0123 D01 K0 D23
M10:1
M00:1
M10:2
M00:2
T2:01
T2:23 C2:01
M10:3 C2:23 L10
M00:3 L00 E10
M01:012 Q2:0123 E00 I1
M11:012 J1
M12:0 P3:0123
M20:0123 K1 L20 J2
M21:012
T3:01
T3:23 I2 C3:01
M21:3
M22:0 P4:0123
M01:3 C3:23
M22:12 L21 E20
M11:3
T4:01 K2
T4:23 J3 Q3:0123
M12:12 E21
M13:0 L01
M22:3 C4:01
M12:3 L11 E01
M13:12 L22 C4:23 L12
M30:0123 E22 L30 E11 P5:0123
M31:0123 E30 Q4:0123 E12
M32:012
T5:01
T5:23 L31 C5:01
M32:3 I3 E31 L32 C5:23
M40:0123 K3 E32
M03:012 Q5:0123 P6:0
M33:012 P6:1 L40
M13:3 P6:2
M03:3 L13 P6:3
M33:3 E40 L03 E13
M02:0123 B6:01 E03 L33 C6:01
M50:0123 B6:23 E33 L02
M23:0123 C6:23 L50 E02
M51:0123 Q6:01 E50 L23 Q6:23
M42:0123 E23 P7:0 L51
M52:0123 P7:1 P7:2 E51 L42
M41:0123 B7:01 E42 L52 C7:01
M60:0123 P7:3 L41 E52 Q7:01
M63:0123 E41 B7:23 L60
M53:0123 C7:23 L63 E60
M62:0123 Q7:23 E63 L53 L62
M61:0123 E53 L61 E62
M43:0123 L43 E61
M70:0123 E43 L70
M71:0123 E70 L71
M72:0123 E71 L72 E72
"""


def tile_dino_teacher_scores_s1_kernel(tc, z_hi, z_lo, w_hi, w_lo_words, w_lo_scales, sharpen, centre, out):
    nc = tc.nc
    with ExitStack() as ctx:
        keep = ctx.enter_context(tc.tile_pool(name="keep", bufs=1))
        work = ctx.enter_context(tc.tile_pool(name="work", bufs=WORK_BUFS))
        outs = ctx.enter_context(tc.tile_pool(name="outs", bufs=OUT_BUFS))
        psum = ctx.enter_context(tc.psum_pool(name="psum", bufs=1))

        def kept(shape, dtype, name):
            return keep.tile(shape, dtype, name=name, align_bytes=256)

        ident = kept([P, P], F32, "ident")
        make_identity(nc, ident[:])

        rows_in = kept([P, 2 * P], BF16, "rows_in")
        sharpen_in = kept([P, P], BF16, "sharpen_in")
        cols = kept([P, 32 + TILES], F32, "cols")
        centre_all = kept([P, N], BF16, "centre_all")
        warm = kept([P, 1], F32, "warm")

        wlo_scales = kept([P, LO, N], U8, "wlo_scales")
        wlo = [kept([P, LO, 2 * W], U8, "wlo0"), kept([P, LO, 2 * (N - W)], U8, "wlo1")]
        whi, whi_grouped, whi_codes, whi_scales = [], [], [], []
        for c in range(CHUNKS):
            whi.append(kept([P, 4, W], BF16, "whi%d" % c))
            whi_grouped.append(kept([P, W, 4], BF16, "whi_grouped%d" % c))
            whi_codes.append(kept([P, W], U32, "whi_codes%d" % c))
            whi_scales.append(kept([P, W], U8, "whi_scales%d" % c))
        zlo, zhi, z_codes, z_scales = [], [], [], []
        for r in range(BLOCK_TILES[0]):
            zlo.append(kept([P, B], BF16, "zlo%d" % r))
            zhi.append(kept([P, A], BF16, "zhi%d" % r))
        z_quarters = kept([P, 4 * len(BLOCK_TILES), PASSES, P], BF16, "z_quarters")
        for r in range(TILES):
            z_codes.append(kept([P, PASSES * P], U32, "z_codes%d" % r))
            z_scales.append(kept([P, PASSES * P], U8, "z_scales%d" % r))
        crops = [slice(P * r, P * (r + 1)) for r in range(TILES)]

        ctx.enter_context(tc.manual_schedule())

        nc.vector.memset(warm[:], 0.0)
        nc.vector.memset(rows_in[:].bitcast(I32), 0)
        nc.vector.memset(sharpen_in[:].bitcast(I32), 0)
        nc.vector.memset(wlo_scales[:].rearrange("p g n -> p (g n)").bitcast(I32), 0)
        nc.scalar.activation(out=warm[:], in_=warm[:], func=EXP)

        whi_rows = w_hi.rearrange("(p j) n -> p j n", j=4)

        def load_zlo(r, lo=0, hi=B):
            nc.sync.dma_start(out=zlo[r][:, lo:hi], in_=z_lo[crops[r], lo:hi])

        def load_zhi(r):
            nc.sync.dma_start(out=zhi[r][:], in_=z_hi[crops[r], :])

        def load_whi(c):
            nc.sync.dma_start(out=whi[c][:], in_=whi_rows[:, :, W * c : W * (c + 1)])

        def load_wlo(i, lo, hi):
            nc.sync.dma_start(
                out=wlo[i][:].bitcast(I32),
                in_=w_lo_words[:, :, 2 * lo : 2 * hi].rearrange("g p n -> p g n").bitcast(I32),
            )

        def load_wlo_scales(lo, hi):
            for q in range(4):
                nc.sync.dma_start(
                    out=wlo_scales[32 * q : 32 * q + 4, :, lo:hi].bitcast(I32),
                    in_=w_lo_scales[:, 4 * q : 4 * q + 4, lo:hi].rearrange("g r n -> r g n").bitcast(I32),
                )

        def load_quarters(g):
            first = P * BLOCK_TILES[0]
            src = z_hi[first:M, :] if g == HI else z_lo[first:M, K_PASS * g : K_PASS * (g + 1)]
            for q in (0, 2, 1, 3):
                nc.sync.dma_start(
                    out=z_quarters[32 * q : 32 * (q + 1), :, g, :],
                    in_=src[:, P * q : P * (q + 1)].rearrange("(b w) k -> w b k", w=32),
                )

        load_zlo(0, 0, K_PASS)
        load_zhi(0)
        load_zlo(0, K_PASS, B)
        load_zlo(1)
        load_wlo(0, 0, W)
        load_wlo_scales(0, W)
        load_zhi(1)
        nc.sync.dma_start(out=rows_in[0:8, :], in_=centre.rearrange("(a b) -> a b", b=2 * P))
        nc.sync.dma_start(out=sharpen_in[32:40, :], in_=sharpen.rearrange("(a b) -> a b", b=P))
        load_whi(0)
        load_zhi(2)
        load_zlo(2)
        load_wlo_scales(W, N)
        load_wlo(1, W, N)
        load_whi(1)
        load_zlo(3)
        load_zhi(3)
        load_whi(2)
        load_zlo(4)
        load_zhi(4)
        load_whi(3)
        load_quarters(0)
        load_zlo(5)
        load_zhi(5)
        load_quarters(1)
        load_quarters(HI)
        load_quarters(2)

        ordered, turned, blocks, grouped, sums, results, spread_out = {}, {}, {}, {}, {}, {}, {}

        def z_words(r, g):
            if g == HI:
                return zhi[r][:].bitcast(F32)
            return zlo[r][:].bitcast(F32)[:, WORDS * g : WORDS * (g + 1)]

        def put_in_order(r, passes):
            if r not in ordered:
                ordered[r] = work.tile([P, PASSES * WORDS], F32, tag="ordered", name="ordered", align_bytes=256)
            copy = nc.scalar.copy if r in PRE_ON_SCALAR else nc.vector.tensor_copy
            if r in BLOCK_TILES:
                b = 4 * (r - BLOCK_TILES[0])
                for g in passes:
                    copy(
                        out=ordered[r][:, WORDS * g : WORDS * (g + 1)].rearrange("p (u b w) -> p u b w", u=2, b=4),
                        in_=z_quarters[:, b : b + 4, g, :].bitcast(F32).rearrange("p b (w u) -> p u b w", u=2),
                    )
                return
            lo_passes = [g for g in passes if g != HI]
            pieces = [(lo_passes[0], lo_passes[-1] + 1, zlo[r])] if lo_passes else []
            if HI in passes:
                pieces.append((HI, HI + 1, zhi[r]))
            for g0, g1, tile in pieces:
                first = 0 if g0 == HI else WORDS * g0
                copy(
                    out=ordered[r][:, WORDS * g0 : WORDS * g1].rearrange("p (g u w) -> p u g w", u=2, w=P),
                    in_=tile[:].bitcast(F32)[:, first : first + WORDS * (g1 - g0)].rearrange(
                        "p (g w u) -> p u g w", u=2, w=P
                    ),
                )

        def transpose(r, passes):
            bank = psum.tile([P, 4, P], F32, tag="turned", name="turned", bufs=8 - ACC_BANKS)
            turned[(r, passes[0])] = bank
            for i, (g, u) in enumerate([(g, u) for g in passes for u in (0, 1)]):
                if r == 0:
                    words = z_words(r, g)[:, u:WORDS:2]
                else:
                    words = ordered[r][:, WORDS * g + P * u : WORDS * g + P * (u + 1)]
                nc.tensor.transpose(bank[:, i, :], words, ident[:])

        def transpose_blocks(r, passes):
            if r not in blocks:
                blocks[r] = work.tile([P, PASSES * WORDS], F32, tag="blocks", name="blocks", align_bytes=256)
            part = slice(WORDS * passes[0], WORDS * (passes[-1] + 1))
            nc.vector.transpose(out=blocks[r][:, part], in_=ordered[r][:, part])

        def group(r, passes):
            if r not in grouped:
                grouped[r] = work.tile([P, PASSES * K_PASS], BF16, tag="grouped", name="grouped", align_bytes=256)
            n = len(passes)
            part = slice(WORDS * passes[0], WORDS * (passes[-1] + 1))
            if r in BLOCK_TILES:
                words = blocks[r][:, part].rearrange("p (g u r) -> p g r u", g=n, u=2)
            else:
                words = turned[(r, passes[0])][:, 0 : 2 * n, :].rearrange("p (g u) r -> p g r u", u=2)
            nc.scalar.copy(
                out=grouped[r][:].bitcast(F32)[:, part].rearrange("p (g r u) -> p g r u", g=n, u=2), in_=words
            )

        def quantise(r, passes):
            first, end = passes[0], passes[-1] + 1
            nc.vector.quantize_mx(
                out=z_codes[r][:, P * first : P * end].bitcast(FP8X4),
                scales=z_scales[r][:, P * first : P * end],
                in_=grouped[r][:, K_PASS * first : K_PASS * end],
            )

        def interleave(c, copy, cols_part):
            copy(
                out=whi_grouped[c][:, cols_part, :], in_=whi[c][:, :, cols_part].rearrange("p j n -> p n j")
            )

        def quantise_whi(c):
            nc.vector.quantize_mx(
                out=whi_codes[c][:].bitcast(FP8X4),
                scales=whi_scales[c][:],
                in_=whi_grouped[c][:].rearrange("p n j -> p (n j)"),
            )

        def vectors_to_columns():
            bank = psum.tile([P, 4, P], F32, tag="turned", name="turned", bufs=8 - ACC_BANKS)
            nc.vector.tensor_copy(out=rows_in[32:64, :].bitcast(F32), in_=sharpen_in[32:64, :])
            nc.tensor.transpose(bank[:, 0, :], rows_in[:].bitcast(F32), ident[:])
            nc.scalar.copy(out=cols[:], in_=bank[:, 0, 0 : 32 + TILES])

        def spread(chunks):
            bank = psum.tile([P, 4, P], F32, tag="turned", name="turned", bufs=8 - ACC_BANKS)
            spread_out[chunks] = bank
            for i in range(4):
                a = 2 * chunks[0] + i
                nc.tensor.transpose(bank[:, i, :], cols[:, a : a + 1].to_broadcast([P, P]), ident[:])

        def copy_spread(chunks):
            nc.scalar.copy(
                out=centre_all[:, W * chunks[0] : W * (chunks[1] + 1)].bitcast(F32),
                in_=spread_out[chunks][:].rearrange("p a b -> p (a b)"),
            )

        def multiply(r, c, passes, lo=0, hi=W):
            if (r, c) not in sums:
                sums[(r, c)] = psum.tile([P, W], F32, tag="sums", name="sums", bufs=ACC_BANKS)
            for g in passes:
                if g == HI:
                    rhs, rhs_scale = whi_codes[c][:, lo:hi].bitcast(FP8X4), whi_scales[c][:, lo:hi]
                else:
                    codes, first = (wlo[0], 0) if c == 0 else (wlo[1], W * (c - 1))
                    rhs = codes[:, g, 2 * (first + lo) : 2 * (first + hi)].bitcast(FP4X4)
                    rhs_scale = wlo_scales[:, g, W * c + lo : W * c + hi]
                nc.tensor.matmul_mx(
                    out=sums[(r, c)][:, lo:hi],
                    lhsT=z_codes[r][:, P * g : P * (g + 1)].bitcast(FP8X4),
                    lhsT_scale=z_scales[r][:, P * g : P * (g + 1)],
                    rhs=rhs,
                    rhs_scale=rhs_scale,
                    start=(g == 0),
                    stop=(g == HI),
                )

        def logits(r, c, lo=0, hi=W):
            if (r, c) not in results:
                results[(r, c)] = outs.tile([P, W], F32, tag="results", name="results", align_bytes=256)
            nc.vector.scalar_tensor_tensor(
                out=results[(r, c)][:, lo:hi],
                in0=sums[(r, c)][:, lo:hi],
                scalar=cols[:, 32 + r : 33 + r],
                in1=centre_all[:, W * c + lo : W * c + hi],
                op0=mybir.AluOpType.mult,
                op1=mybir.AluOpType.subtract,
            )

        def exp(r, c, lo=0, hi=W):
            part = results[(r, c)][:, lo:hi]
            nc.scalar.activation(out=part, in_=part, func=EXP)

        def store(r, c, lo=0, hi=W):
            nc.sync.dma_start(out=out[crops[r], W * c + lo : W * c + hi], in_=results[(r, c)][:, lo:hi])

        def exp_and_store(r, c):
            exp(r, c)
            store(r, c)

        by_tile = {"P": put_in_order, "T": transpose, "B": transpose_blocks, "C": group, "Q": quantise}
        for step in PLAN.split():
            kind, (head, *rest) = step[0], step[1:].split(":")
            passes = [int(g) for g in rest[0]] if rest else []
            where = tuple([int(x) for x in head])
            if kind in by_tile:
                by_tile[kind](where[0], passes)
            elif kind == "M":
                multiply(where[0], where[1], passes)
            elif kind == "L":
                logits(where[0], where[1])
            elif kind == "E":
                exp_and_store(where[0], where[1])
            elif kind == "I":
                interleave(where[0], nc.vector.tensor_copy, slice(0, W_ON_VECTOR))
            elif kind == "J":
                interleave(where[0], nc.scalar.copy, slice(W_ON_VECTOR, W))
            elif kind == "K":
                quantise_whi(where[0])
            elif kind == "V":
                vectors_to_columns()
            elif kind == "S":
                spread(where)
            else:
                copy_spread(where)

        r, c = TILES - 1, CHUNKS - 1
        for lo in range(0, W, P):
            multiply(r, c, range(PASSES), lo, lo + P)
        parts = ((0, 2 * P), (2 * P, 3 * P), (3 * P, W))
        for lo, hi in parts:
            logits(r, c, lo, hi)
        for lo, hi in parts:
            exp(r, c, lo, hi)
        for lo, hi in ((0, 2 * P), (2 * P, W)):
            store(r, c, lo, hi)
